import numpy as np
import ml_dtypes


def mxq(x, axis, fmt="e4m3"):
    dtype, down = {"e4m3": (ml_dtypes.float8_e4m3fn, 7), "e5m2": (ml_dtypes.float8_e5m2, 14)}[fmt]
    v = np.moveaxis(np.asarray(x, np.float32).astype(ml_dtypes.bfloat16).astype(np.float64), axis, -1)
    blocks = v.reshape(v.shape[:-1] + (-1, 32))
    amax = np.abs(blocks).max(-1, keepdims=True)
    byte = np.maximum(np.where(amax > 0, np.frexp(amax)[1] - 1 + 127, 0) - down, 1)
    scale = np.exp2(byte - 127.0)
    codes = (blocks / scale).astype(np.float32).astype(dtype).astype(np.float64)
    return np.moveaxis((codes * scale).reshape(v.shape), -1, axis)


WIDE = False


def mx_kscale(k):
    if not WIDE:
        return np.ones(k)
    levels = np.array([10, -10, 5, -5, 0])
    if k % 512:
        return np.exp2(np.random.permutation(np.resize(levels, k // 32))).repeat(32)
    a = np.empty((k // 512, 16))
    for p in range(k // 512):
        a[p, :8] = np.random.permutation(np.resize(levels, 8))
        for g in range(8):
            far = levels[np.abs(levels - a[p, g]) >= 10]
            a[p, g + 8] = far[np.random.randint(len(far))]
    return np.exp2(a.ravel()).repeat(32)


def f64(x):
    return np.asarray(x).astype(np.float64)


def striped(idx):
    return np.tile(np.asarray(idx).reshape(-1, 16).T, (8, 1)).astype(np.uint16)


def unstriped(offs):
    return offs[:16].T.reshape(-1).astype(np.int64)


E2M1 = np.array([0.0, 0.5, 1.0, 1.5, 2.0, 3.0, 4.0, 6.0, -0.0, -0.5, -1.0, -1.5, -2.0, -3.0, -4.0, -6.0])


def pack_weight(w, fmt):
    k, n = w.shape
    w = f64(np.asarray(w, np.float32).astype(ml_dtypes.bfloat16)).reshape(k // 32, 32, n)
    amax = np.abs(w).max(1)
    if fmt == "e4m3":
        byte = np.frexp(amax)[1] - 1 + 127 - 7
    else:
        mant, ex = np.frexp(amax / 6.0)
        byte = np.where(mant > 0.5, ex, ex - 1) + 127
    byte = np.clip(np.where(amax > 0, byte, 1), 1, 254)
    scaled = (w * np.exp2(127.0 - byte)[:, None, :]).reshape(k, n).astype(np.float32)
    by_word = np.ascontiguousarray(scaled.reshape(k // 512, 128, 4, n).transpose(0, 1, 3, 2))
    if fmt == "e4m3":
        words = by_word.astype(ml_dtypes.float8_e4m3fn).view(np.uint8)
    else:
        c = by_word.astype(ml_dtypes.float4_e2m1fn).view(np.uint8) & 0xF
        words = (c[..., 0::2] | (c[..., 1::2] << 4)).reshape(k // 512, 128, 2 * n)
    return np.ascontiguousarray(words), np.ascontiguousarray(byte.astype(np.uint8).reshape(k // 512, 16, n))


def unpack_weight(words, scales, fmt):
    g, _, n = scales.shape
    words = np.ascontiguousarray(words).reshape(g, 128, n, -1)
    if fmt == "e4m3":
        vals = words.view(ml_dtypes.float8_e4m3fn).astype(np.float64)
    else:
        nib = np.empty((g, 128, n, 4), np.uint8)
        nib[..., 0::2] = words & 0xF
        nib[..., 1::2] = words >> 4
        vals = E2M1[nib]
    vals = vals * np.repeat(np.exp2(scales.astype(np.float64) - 127.0), 8, axis=1)[..., None]
    return vals.transpose(0, 1, 3, 2).reshape(g * 512, n)


B, N, T, D, DV, NQ = 1, 1024, 4096, 1024, 0, 256
PAGE = 64
SEG = 64


def setup_inputs():
    n = np.random.standard_normal
    pages = np.random.permutation(T // PAGE)[:B * N // PAGE]
    idx = (pages[:, None] * PAGE + np.arange(PAGE)[None, :]).reshape(-1)
    s = mx_kscale(D)[:, None]
    r = np.random.uniform(0.5, 2.0, T)
    kp = pack_weight(n((D, T)) / s / r, "e2m1")
    return {
        "qT": (n((B, D, NQ)) * s * (1.00 / np.sqrt(D))).astype(np.float32),
        "k_words": np.ascontiguousarray(kp[0].reshape(1, 2, 128, T, 2).transpose(0, 2, 3, 1, 4)).reshape(1, 128, T, 4),
        "k_scales": kp[1],
        "ts": np.tile(r, (128, 1)).astype(np.float32),
        "offs": striped(idx),
    }


def reference(qT, k_words, k_scales, ts, offs):
    idx = unstriped(offs)
    pool = unpack_weight(k_words.reshape(1, 128, T, 2, 2).transpose(0, 3, 1, 2, 4).reshape(2, 128, 2 * T), k_scales, "e2m1")
    pick = lambda x: x[:, idx].reshape(x.shape[0], B, N).transpose(1, 0, 2)
    a = mxq(f64(qT), 1, "e4m3").transpose(0, 2, 1) @ pick(pool)
    a = a * pick(f64(ts))[:, :1, :]
    return a.reshape(B, NQ, N // SEG, SEG).max(-1)

@@ -1,0 +1,166 @@
+from contextlib import ExitStack
+
+import concourse.mybir as mybir
+from concourse.masks import make_identity
+
+F32 = mybir.dt.float32
+BF16 = mybir.dt.bfloat16
+I32 = mybir.dt.int32
+U32 = mybir.dt.uint32
+U16 = mybir.dt.uint16
+U8 = mybir.dt.uint8
+FP8X4 = mybir.dt.float8_e4m3fn_x4
+FP4X4 = mybir.dt.float4_e2m1fn_x4
+COPY = mybir.ActivationFunctionType.Copy
+MULT = mybir.AluOpType.mult
+MAX = mybir.AluOpType.max
+
+P = 128
+POOL = 4096
+SLOTS = 1024
+D = 1024
+NQ = 256
+SEG = 64
+PASSES = 2
+PACK = 4
+HALVES = 2
+HALF = SLOTS // HALVES
+BLOCKS = HALF // P
+RUN = SEG // BLOCKS
+SEGS = HALF // SEG
+QT = NQ // P
+LIST_COLS = HALF // 16
+
+FLOPS = 2 * NQ * SLOTS * D
+BYTES = 4 * D * NQ + 4 * P * POOL + 32 * POOL + 4 * POOL + 2 * P * SLOTS // 16 + 4 * NQ * 16
+
+
+def tile_attend_maxsim_ts_kernel(tc, qT, k_words, k_scales, ts, offs, out):
+    nc = tc.nc
+    with ExitStack() as ctx:
+        keep = ctx.enter_context(tc.tile_pool(name="keep", bufs=1))
+        score_psum = ctx.enter_context(tc.psum_pool(name="score_psum", bufs=6))
+        turn_psum = ctx.enter_context(tc.psum_pool(name="turn_psum", bufs=2))
+
+        offsets = keep.tile([P, SLOTS // 16], U16, name="offsets")
+        nc.sync.dma_start(offsets[:], offs)
+
+        scale_pool = keep.tile([P, POOL], U8, name="scale_pool", align_bytes=64)
+        nc.sync.dma_start(
+            scale_pool[0:32, :].bitcast(I32),
+            k_scales.rearrange("o f t -> (o f) t").bitcast(I32),
+        )
+        q_raw = []
+        for o in range(PASSES):
+            raw = keep.tile([P, PACK, NQ], F32, name="q_raw%d" % o)
+            nc.sync.dma_start(raw[:], qT[0, 512 * o : 512 * (o + 1), :].rearrange("(p j) w -> p j w", j=PACK))
+            q_raw.append(raw)
+        word_pool = keep.tile([P, POOL], I32, name="word_pool", align_bytes=64)
+        nc.sync.dma_start(word_pool[:], k_words[0].rearrange("p t b -> p (t b)").bitcast(I32))
+
+        nc.vector.memset(scale_pool[32:64, :].bitcast(I32), 0)
+        nc.vector.memset(scale_pool[64:128, :].bitcast(I32), 0)
+        ts_pool = keep.tile([P, POOL], F32, name="ts_pool", align_bytes=64)
+        nc.vector.memset(ts_pool[:], 0.0)
+        nc.gpsimd.dma_start(ts_pool[0:1, :], ts[0:1, :])
+        identity = keep.tile([P, P], F32, name="identity")
+        make_identity(nc, identity[:])
+
+        scale_listed = keep.tile([P, SLOTS], U8, name="scale_listed", align_bytes=64)
+        nc.vector.tensor_copy(scale_listed[:], scale_pool[:].indirect(offsets[:]))
+        planes = [keep.tile([P, SLOTS], U8, name="plane%d" % o, align_bytes=64) for o in range(PASSES)]
+        nc.vector.memset(planes[1][:].bitcast(I32), 0)
+        for h in range(HALVES):
+            cols = slice(h * HALF, (h + 1) * HALF)
+            nc.vector.tensor_copy(
+                planes[0][:, cols].rearrange("p (b j r) -> p b j r", b=BLOCKS, r=RUN),
+                scale_listed[:, cols].rearrange("p (j b r) -> p b j r", b=BLOCKS, r=RUN),
+            )
+
+        q_codes = keep.tile([P, PASSES, NQ], U32, name="q_codes", align_bytes=64)
+        q_scales = keep.tile([P, PASSES, NQ], U8, name="q_scales", align_bytes=64)
+        q_bf = []
+        for o in range(PASSES):
+            grouped = keep.tile([P, NQ, PACK], BF16, name="q_bf%d" % o, align_bytes=64)
+            nc.scalar.activation(grouped[:], q_raw[o][:].rearrange("p j w -> p w j"), COPY)
+            q_bf.append(grouped)
+            if o == 0:
+                for po in range(PASSES):
+                    for quad in range(4):
+                        if po == 0 and quad == 0:
+                            continue
+                        first = 16 * po + 4 * quad
+                        nc.scalar.dma_start(
+                            planes[po][32 * quad : 32 * quad + 4, :].bitcast(I32),
+                            planes[0][first : first + 4, :].bitcast(I32),
+                        )
+        for o in range(PASSES):
+            nc.vector.quantize_mx(
+                out=q_codes[:, o, :].bitcast(FP8X4),
+                scales=q_scales[:, o, :],
+                in_=q_bf[o][:].rearrange("p w j -> p (w j)"),
+            )
+
+        ts_listed = keep.tile([P, SLOTS], F32, name="ts_listed", align_bytes=64)
+        nc.vector.tensor_copy(ts_listed[:], ts_pool[:].indirect(offsets[:]))
+        ts_blocks = keep.tile([P, SLOTS], F32, name="ts_blocks", align_bytes=64)
+        ts_col = keep.tile([P, HALVES * BLOCKS], F32, name="ts_col")
+        for h in range(HALVES):
+            cols = slice(h * HALF, (h + 1) * HALF)
+            nc.scalar.copy(
+                ts_blocks[:, cols].rearrange("p (b j r) -> p b j r", b=BLOCKS, r=RUN),
+                ts_listed[:, cols].rearrange("p (j b r) -> p b j r", b=BLOCKS, r=RUN),
+            )
+            turned = turn_psum.tile([P, BLOCKS, P], F32, name="turned")
+            for b in range(BLOCKS):
+                first = h * HALF + b * P
+                nc.tensor.transpose(turned[:, b, :], ts_blocks[:, first : first + P], identity[:])
+            nc.scalar.copy(ts_col[:, h * BLOCKS : (h + 1) * BLOCKS], turned[:, :, 0])
+
+        key_codes = []
+        for h in range(HALVES):
+            listed = keep.tile([P, HALF], U32, name="word_listed%d" % h, align_bytes=64)
+            nc.vector.tensor_copy(
+                listed[:],
+                word_pool[:].bitcast(U32).indirect(offsets[:, h * LIST_COLS : (h + 1) * LIST_COLS]),
+            )
+            by_block = listed[:].bitcast(U16).rearrange("p (j b r o) -> p b o j r", b=BLOCKS, r=RUN, o=PASSES)
+            for b in range(BLOCKS):
+                codes = keep.tile([P, PASSES, P], U16, name="key_codes%d_%d" % (h, b), align_bytes=64)
+                nc.vector.tensor_copy(codes[:].rearrange("p o (j r) -> p o j r", r=RUN), by_block[:, b])
+                key_codes.append(codes)
+
+        result = keep.tile([P, QT, HALVES * SEGS], F32, name="result")
+        for h in range(HALVES):
+            best = keep.tile([P, NQ], F32, name="best%d" % h)
+            for b in range(BLOCKS):
+                block = h * BLOCKS + b
+                key_cols = slice(block * P, (block + 1) * P)
+                scores = score_psum.tile([P, NQ], F32, name="scores")
+                for qt in range(QT):
+                    q_cols = slice(qt * P, (qt + 1) * P)
+                    for o in range(PASSES):
+                        nc.tensor.matmul_mx(
+                            out=scores[:, q_cols],
+                            lhsT=key_codes[block][:, o, :].bitcast(FP4X4),
+                            lhsT_scale=planes[o][:, key_cols],
+                            rhs=q_codes[:, o, q_cols].bitcast(FP8X4),
+                            rhs_scale=q_scales[:, o, q_cols],
+                            start=(o == 0),
+                            stop=(o == PASSES - 1),
+                        )
+                factor = ts_col[:, block : block + 1]
+                if b == 0:
+                    nc.scalar.activation(best[:], scores[:], COPY, scale=factor)
+                else:
+                    nc.vector.scalar_tensor_tensor(best[:], scores[:], factor, best[:], MULT, MAX)
+            turned = turn_psum.tile([P, BLOCKS, P], F32, name="turned")
+            for qt in range(QT):
+                nc.tensor.transpose(turned[:, qt, :], best[:, qt * P : (qt + 1) * P], identity[:])
+            nc.vector.tensor_reduce(
+                result[:, :, h * SEGS : (h + 1) * SEGS],
+                turned[:, 0:QT, :].rearrange("p t (j r) -> p t j r", r=RUN),
+                mybir.AxisListType.X,
+                MAX,
+            )
+        nc.sync.dma_start(out[0].rearrange("(t p) j -> p t j", p=P), result[:])

@@ -50,19 +50,20 @@ def tile_attend_maxsim_ts_kernel(tc, qT, k_words, k_scales, ts, offs, out):
             scale_pool[0:32, :].bitcast(I32),
             k_scales.rearrange("o f t -> (o f) t").bitcast(I32),
         )
+        ts_pool = keep.tile([P, POOL], F32, name="ts_pool", align_bytes=64)
         q_raw = []
         for o in range(PASSES):
             raw = keep.tile([P, PACK, NQ], F32, name="q_raw%d" % o)
             nc.sync.dma_start(raw[:], qT[0, 512 * o : 512 * (o + 1), :].rearrange("(p j) w -> p j w", j=PACK))
             q_raw.append(raw)
+            if o == 0:
+                nc.sync.dma_start(ts_pool[P - 1 : P, :], ts[0:1, :])
         word_pool = keep.tile([P, POOL], I32, name="word_pool", align_bytes=64)
         nc.sync.dma_start(word_pool[:], k_words[0].rearrange("p t b -> p (t b)").bitcast(I32))
 
         nc.vector.memset(scale_pool[32:64, :].bitcast(I32), 0)
         nc.vector.memset(scale_pool[64:128, :].bitcast(I32), 0)
-        ts_pool = keep.tile([P, POOL], F32, name="ts_pool", align_bytes=64)
-        nc.vector.memset(ts_pool[:], 0.0)
-        nc.gpsimd.dma_start(ts_pool[0:1, :], ts[0:1, :])
+        nc.vector.memset(ts_pool[0 : P - 1, :], 0.0)
         identity = keep.tile([P, P], F32, name="identity")
         make_identity(nc, identity[:])
 
@@ -77,12 +78,18 @@ def tile_attend_maxsim_ts_kernel(tc, qT, k_words, k_scales, ts, offs, out):
                 scale_listed[:, cols].rearrange("p (j b r) -> p b j r", b=BLOCKS, r=RUN),
             )
 
+        ts_listed = keep.tile([P, SLOTS], F32, name="ts_listed", align_bytes=64)
+        nc.vector.tensor_copy(ts_listed[:], ts_pool[:].indirect(offsets[:]))
+
         q_codes = keep.tile([P, PASSES, NQ], U32, name="q_codes", align_bytes=64)
         q_scales = keep.tile([P, PASSES, NQ], U8, name="q_scales", align_bytes=64)
         q_bf = []
         for o in range(PASSES):
             grouped = keep.tile([P, NQ, PACK], BF16, name="q_bf%d" % o, align_bytes=64)
-            nc.scalar.activation(grouped[:], q_raw[o][:].rearrange("p j w -> p w j"), COPY)
+            if o == 0:
+                nc.scalar.activation(grouped[:], q_raw[o][:].rearrange("p j w -> p w j"), COPY)
+            else:
+                nc.vector.tensor_copy(grouped[:], q_raw[o][:].rearrange("p j w -> p w j"))
             q_bf.append(grouped)
             if o == 0:
                 for po in range(PASSES):
@@ -101,8 +108,6 @@ def tile_attend_maxsim_ts_kernel(tc, qT, k_words, k_scales, ts, offs, out):
                 in_=q_bf[o][:].rearrange("p w j -> p (w j)"),
             )
 
-        ts_listed = keep.tile([P, SLOTS], F32, name="ts_listed", align_bytes=64)
-        nc.vector.tensor_copy(ts_listed[:], ts_pool[:].indirect(offsets[:]))
         ts_blocks = keep.tile([P, SLOTS], F32, name="ts_blocks", align_bytes=64)
         ts_col = keep.tile([P, HALVES * BLOCKS], F32, name="ts_col")
         for h in range(HALVES):
@@ -115,7 +120,7 @@ def tile_attend_maxsim_ts_kernel(tc, qT, k_words, k_scales, ts, offs, out):
             for b in range(BLOCKS):
                 first = h * HALF + b * P
                 nc.tensor.transpose(turned[:, b, :], ts_blocks[:, first : first + P], identity[:])
-            nc.scalar.copy(ts_col[:, h * BLOCKS : (h + 1) * BLOCKS], turned[:, :, 0])
+            nc.scalar.copy(ts_col[:, h * BLOCKS : (h + 1) * BLOCKS], turned[:, :, P - 1])
 
         key_codes = []
         for h in range(HALVES):

@@ -30,6 +30,7 @@ RUN = SEG // BLOCKS
 SEGS = HALF // SEG
 QT = NQ // P
 LIST_COLS = HALF // 16
+CHAIN = (2, 4)
 
 FLOPS = 2 * NQ * SLOTS * D
 BYTES = 4 * D * NQ + 4 * P * POOL + 32 * POOL + 4 * POOL + 2 * P * SLOTS // 16 + 4 * NQ * 16
@@ -51,13 +52,12 @@ def tile_attend_maxsim_ts_kernel(tc, qT, k_words, k_scales, ts, offs, out):
             k_scales.rearrange("o f t -> (o f) t").bitcast(I32),
         )
         ts_pool = keep.tile([P, POOL], F32, name="ts_pool", align_bytes=64)
+        nc.sync.dma_start(ts_pool[P - 1 : P, :], ts[0:1, :])
         q_raw = []
         for o in range(PASSES):
             raw = keep.tile([P, PACK, NQ], F32, name="q_raw%d" % o)
             nc.sync.dma_start(raw[:], qT[0, 512 * o : 512 * (o + 1), :].rearrange("(p j) w -> p j w", j=PACK))
             q_raw.append(raw)
-            if o == 0:
-                nc.sync.dma_start(ts_pool[P - 1 : P, :], ts[0:1, :])
         word_pool = keep.tile([P, POOL], I32, name="word_pool", align_bytes=64)
         nc.sync.dma_start(word_pool[:], k_words[0].rearrange("p t b -> p (t b)").bitcast(I32))
 
@@ -71,101 +71,97 @@ def tile_attend_maxsim_ts_kernel(tc, qT, k_words, k_scales, ts, offs, out):
         nc.vector.tensor_copy(scale_listed[:], scale_pool[:].indirect(offsets[:]))
         planes = [keep.tile([P, SLOTS], U8, name="plane%d" % o, align_bytes=64) for o in range(PASSES)]
         nc.vector.memset(planes[1][:].bitcast(I32), 0)
-        for h in range(HALVES):
-            cols = slice(h * HALF, (h + 1) * HALF)
-            nc.vector.tensor_copy(
-                planes[0][:, cols].rearrange("p (b j r) -> p b j r", b=BLOCKS, r=RUN),
-                scale_listed[:, cols].rearrange("p (j b r) -> p b j r", b=BLOCKS, r=RUN),
-            )
+        nc.vector.tensor_copy(
+            planes[0][:].bitcast(I32).rearrange("p (b j w) -> p b j w", b=BLOCKS, w=RUN // 4),
+            scale_listed[:].bitcast(I32).rearrange("p (j b w) -> p b j w", b=BLOCKS, w=RUN // 4),
+        )
+        for po in reversed(range(PASSES)):
+            for quad in range(4):
+                if po == 0 and quad == 0:
+                    continue
+                first = 16 * po + 4 * quad
+                nc.sync.dma_start(
+                    planes[po][32 * quad : 32 * quad + 4, :].bitcast(I32),
+                    planes[0][first : first + 4, :].bitcast(I32),
+                )
 
         ts_listed = keep.tile([P, SLOTS], F32, name="ts_listed", align_bytes=64)
-        nc.vector.tensor_copy(ts_listed[:], ts_pool[:].indirect(offsets[:]))
+        nc.vector.tensor_copy(
+            ts_listed[:].bitcast(U32).rearrange("p (b j r) -> p j b r", b=BLOCKS, r=RUN),
+            ts_pool[:].bitcast(U32).indirect(offsets[:]),
+        )
 
         q_codes = keep.tile([P, PASSES, NQ], U32, name="q_codes", align_bytes=64)
         q_scales = keep.tile([P, PASSES, NQ], U8, name="q_scales", align_bytes=64)
-        q_bf = []
         for o in range(PASSES):
             grouped = keep.tile([P, NQ, PACK], BF16, name="q_bf%d" % o, align_bytes=64)
-            if o == 0:
-                nc.scalar.activation(grouped[:], q_raw[o][:].rearrange("p j w -> p w j"), COPY)
-            else:
-                nc.vector.tensor_copy(grouped[:], q_raw[o][:].rearrange("p j w -> p w j"))
-            q_bf.append(grouped)
-            if o == 0:
-                for po in range(PASSES):
-                    for quad in range(4):
-                        if po == 0 and quad == 0:
-                            continue
-                        first = 16 * po + 4 * quad
-                        nc.scalar.dma_start(
-                            planes[po][32 * quad : 32 * quad + 4, :].bitcast(I32),
-                            planes[0][first : first + 4, :].bitcast(I32),
-                        )
-        for o in range(PASSES):
+            nc.scalar.activation(grouped[:], q_raw[o][:].rearrange("p j w -> p w j"), COPY)
             nc.vector.quantize_mx(
                 out=q_codes[:, o, :].bitcast(FP8X4),
                 scales=q_scales[:, o, :],
-                in_=q_bf[o][:].rearrange("p w j -> p (w j)"),
+                in_=grouped[:].rearrange("p w j -> p (w j)"),
             )
 
-        ts_blocks = keep.tile([P, SLOTS], F32, name="ts_blocks", align_bytes=64)
-        ts_col = keep.tile([P, HALVES * BLOCKS], F32, name="ts_col")
+        ts_col = keep.tile([P, HALVES, BLOCKS], F32, name="ts_col")
         for h in range(HALVES):
-            cols = slice(h * HALF, (h + 1) * HALF)
-            nc.scalar.copy(
-                ts_blocks[:, cols].rearrange("p (b j r) -> p b j r", b=BLOCKS, r=RUN),
-                ts_listed[:, cols].rearrange("p (j b r) -> p b j r", b=BLOCKS, r=RUN),
-            )
             turned = turn_psum.tile([P, BLOCKS, P], F32, name="turned")
             for b in range(BLOCKS):
-                first = h * HALF + b * P
-                nc.tensor.transpose(turned[:, b, :], ts_blocks[:, first : first + P], identity[:])
-            nc.scalar.copy(ts_col[:, h * BLOCKS : (h + 1) * BLOCKS], turned[:, :, P - 1])
+                first = (b * HALVES + h) * P
+                nc.tensor.transpose(turned[:, b, :], ts_listed[:, first : first + P], identity[:])
+            nc.scalar.copy(ts_col[:, h, :], turned[:, :, P - 1])
 
         key_codes = []
+        word_listed = keep.tile([P, HALF + P], U32, name="word_listed", align_bytes=64)
         for h in range(HALVES):
-            listed = keep.tile([P, HALF], U32, name="word_listed%d" % h, align_bytes=64)
+            start = P * (HALVES - 1 - h)
             nc.vector.tensor_copy(
-                listed[:],
+                word_listed[:, start : start + HALF].rearrange("p (b j r) -> p j b r", b=BLOCKS, r=RUN),
                 word_pool[:].bitcast(U32).indirect(offsets[:, h * LIST_COLS : (h + 1) * LIST_COLS]),
             )
-            by_block = listed[:].bitcast(U16).rearrange("p (j b r o) -> p b o j r", b=BLOCKS, r=RUN, o=PASSES)
             for b in range(BLOCKS):
                 codes = keep.tile([P, PASSES, P], U16, name="key_codes%d_%d" % (h, b), align_bytes=64)
-                nc.vector.tensor_copy(codes[:].rearrange("p o (j r) -> p o j r", r=RUN), by_block[:, b])
+                words = word_listed[:, start + b * P : start + (b + 1) * P]
+                nc.vector.tensor_copy(codes[:], words.bitcast(U16).rearrange("p (n o) -> p o n", o=PASSES))
                 key_codes.append(codes)
 
         result = keep.tile([P, QT, HALVES * SEGS], F32, name="result")
+        joined = []
         for h in range(HALVES):
-            best = keep.tile([P, NQ], F32, name="best%d" % h)
+            chain = CHAIN[h]
+            best = keep.tile([P, BLOCKS // chain, NQ], F32, name="best%d" % h)
+            joined.append(best)
             for b in range(BLOCKS):
-                block = h * BLOCKS + b
-                key_cols = slice(block * P, (block + 1) * P)
+                first = (b * HALVES + h) * P
+                key_cols = slice(first, first + P)
                 scores = score_psum.tile([P, NQ], F32, name="scores")
                 for qt in range(QT):
                     q_cols = slice(qt * P, (qt + 1) * P)
                     for o in range(PASSES):
                         nc.tensor.matmul_mx(
                             out=scores[:, q_cols],
-                            lhsT=key_codes[block][:, o, :].bitcast(FP4X4),
+                            lhsT=key_codes[h * BLOCKS + b][:, o, :].bitcast(FP4X4),
                             lhsT_scale=planes[o][:, key_cols],
                             rhs=q_codes[:, o, q_cols].bitcast(FP8X4),
                             rhs_scale=q_scales[:, o, q_cols],
                             start=(o == 0),
                             stop=(o == PASSES - 1),
                         )
-                factor = ts_col[:, block : block + 1]
-                if b == 0:
-                    nc.scalar.activation(best[:], scores[:], COPY, scale=factor)
+                factor = ts_col[:, h, b : b + 1]
+                into = best[:, b // chain, :]
+                if b % chain == 0:
+                    nc.scalar.activation(into, scores[:], COPY, scale=factor)
                 else:
-                    nc.vector.scalar_tensor_tensor(best[:], scores[:], factor, best[:], MULT, MAX)
+                    nc.vector.scalar_tensor_tensor(into, scores[:], factor, into, MULT, MAX)
+        for h in range(HALVES):
+            parts = BLOCKS // CHAIN[h]
             turned = turn_psum.tile([P, BLOCKS, P], F32, name="turned")
-            for qt in range(QT):
-                nc.tensor.transpose(turned[:, qt, :], best[:, qt * P : (qt + 1) * P], identity[:])
+            for c in range(parts):
+                for qt in range(QT):
+                    nc.tensor.transpose(turned[:, qt * parts + c, :], joined[h][:, c, qt * P : (qt + 1) * P], identity[:])
             nc.vector.tensor_reduce(
                 result[:, :, h * SEGS : (h + 1) * SEGS],
-                turned[:, 0:QT, :].rearrange("p t (j r) -> p t j r", r=RUN),
-                mybir.AxisListType.X,
+                turned[:, 0 : QT * parts, :].rearrange("p (t c) (j r) -> p t j c r", c=parts, r=RUN),
+                mybir.AxisListType.XY,
                 MAX,
             )
         nc.sync.dma_start(out[0].rearrange("(t p) j -> p t j", p=P), result[:])

@@ -30,7 +30,9 @@ RUN = SEG // BLOCKS
 SEGS = HALF // SEG
 QT = NQ // P
 LIST_COLS = HALF // 16
-CHAIN = (2, 4)
+CHAIN = (2, 2)
+WARM = 2
+PARTING = ((0, 1), (1, 3), (3, 4))
 
 FLOPS = 2 * NQ * SLOTS * D
 BYTES = 4 * D * NQ + 4 * P * POOL + 32 * POOL + 4 * POOL + 2 * P * SLOTS // 16 + 4 * NQ * 16
@@ -40,8 +42,7 @@ def tile_attend_maxsim_ts_kernel(tc, qT, k_words, k_scales, ts, offs, out):
     nc = tc.nc
     with ExitStack() as ctx:
         keep = ctx.enter_context(tc.tile_pool(name="keep", bufs=1))
-        score_psum = ctx.enter_context(tc.psum_pool(name="score_psum", bufs=6))
-        turn_psum = ctx.enter_context(tc.psum_pool(name="turn_psum", bufs=2))
+        psum = ctx.enter_context(tc.psum_pool(name="psum", bufs=8))
 
         offsets = keep.tile([P, SLOTS // 16], U16, name="offsets")
         nc.sync.dma_start(offsets[:], offs)
@@ -104,7 +105,7 @@ def tile_attend_maxsim_ts_kernel(tc, qT, k_words, k_scales, ts, offs, out):
 
         ts_col = keep.tile([P, HALVES, BLOCKS], F32, name="ts_col")
         for h in range(HALVES):
-            turned = turn_psum.tile([P, BLOCKS, P], F32, name="turned")
+            turned = psum.tile([P, BLOCKS, P], F32, name="bank")
             for b in range(BLOCKS):
                 first = (b * HALVES + h) * P
                 nc.tensor.transpose(turned[:, b, :], ts_listed[:, first : first + P], identity[:])
@@ -118,11 +119,23 @@ def tile_attend_maxsim_ts_kernel(tc, qT, k_words, k_scales, ts, offs, out):
                 word_listed[:, start : start + HALF].rearrange("p (b j r) -> p j b r", b=BLOCKS, r=RUN),
                 word_pool[:].bitcast(U32).indirect(offsets[:, h * LIST_COLS : (h + 1) * LIST_COLS]),
             )
-            for b in range(BLOCKS):
-                codes = keep.tile([P, PASSES, P], U16, name="key_codes%d_%d" % (h, b), align_bytes=64)
-                words = word_listed[:, start + b * P : start + (b + 1) * P]
+            for b0, b1 in PARTING:
+                codes = keep.tile([P, PASSES, (b1 - b0) * P], U16, name="key_codes%d_%d" % (h, b0), align_bytes=64)
+                words = word_listed[:, start + b0 * P : start + b1 * P]
                 nc.vector.tensor_copy(codes[:], words.bitcast(U16).rearrange("p (n o) -> p o n", o=PASSES))
-                key_codes.append(codes)
+                key_codes.extend(codes[:, :, i * P : (i + 1) * P] for i in range(b1 - b0))
+
+        idle = psum.tile([P, PASSES * NQ], F32, name="bank")
+        for i in range(WARM):
+            nc.tensor.matmul_mx(
+                out=idle[:],
+                lhsT=word_pool[:, 0 : P // 2].bitcast(FP4X4),
+                lhsT_scale=scale_pool[:, 0:P],
+                rhs=q_codes[:].rearrange("p o n -> p (o n)").bitcast(FP8X4),
+                rhs_scale=q_scales[:].rearrange("p o n -> p (o n)"),
+                start=True,
+                stop=True,
+            )
 
         result = keep.tile([P, QT, HALVES * SEGS], F32, name="result")
         joined = []
@@ -133,7 +146,7 @@ def tile_attend_maxsim_ts_kernel(tc, qT, k_words, k_scales, ts, offs, out):
             for b in range(BLOCKS):
                 first = (b * HALVES + h) * P
                 key_cols = slice(first, first + P)
-                scores = score_psum.tile([P, NQ], F32, name="scores")
+                scores = psum.tile([P, NQ], F32, name="bank")
                 for qt in range(QT):
                     q_cols = slice(qt * P, (qt + 1) * P)
                     for o in range(PASSES):
@@ -154,7 +167,7 @@ def tile_attend_maxsim_ts_kernel(tc, qT, k_words, k_scales, ts, offs, out):
                     nc.vector.scalar_tensor_tensor(into, scores[:], factor, into, MULT, MAX)
         for h in range(HALVES):
             parts = BLOCKS // CHAIN[h]
-            turned = turn_psum.tile([P, BLOCKS, P], F32, name="turned")
+            turned = psum.tile([P, BLOCKS, P], F32, name="bank")
             for c in range(parts):
                 for qt in range(QT):
                     nc.tensor.transpose(turned[:, qt * parts + c, :], joined[h][:, c, qt * P : (qt + 1) * P], identity[:])

@@ -32,7 +32,11 @@ QT = NQ // P
 LIST_COLS = HALF // 16
 CHAIN = (2, 2)
 WARM = 2
-PARTING = ((0, 1), (1, 3), (3, 4))
+WHOLE = ((0, SEGS),)
+PARTING = (
+    (((0, 1), WHOLE), ((1, 4), ((0, 6), (6, 8)))),
+    (((0, 1), WHOLE), ((1, 2), WHOLE), ((2, 4), WHOLE)),
+)
 
 FLOPS = 2 * NQ * SLOTS * D
 BYTES = 4 * D * NQ + 4 * P * POOL + 32 * POOL + 4 * POOL + 2 * P * SLOTS // 16 + 4 * NQ * 16
@@ -96,7 +100,11 @@ def tile_attend_maxsim_ts_kernel(tc, qT, k_words, k_scales, ts, offs, out):
         q_scales = keep.tile([P, PASSES, NQ], U8, name="q_scales", align_bytes=64)
         for o in range(PASSES):
             grouped = keep.tile([P, NQ, PACK], BF16, name="q_bf%d" % o, align_bytes=64)
-            nc.scalar.activation(grouped[:], q_raw[o][:].rearrange("p j w -> p w j"), COPY)
+            nc.scalar.activation(
+                grouped[:].rearrange("p (c i) j -> p c j i", i=2),
+                q_raw[o][:].rearrange("p j (c i) -> p c j i", i=2),
+                COPY,
+            )
             nc.vector.quantize_mx(
                 out=q_codes[:, o, :].bitcast(FP8X4),
                 scales=q_scales[:, o, :],
@@ -115,15 +123,18 @@ def tile_attend_maxsim_ts_kernel(tc, qT, k_words, k_scales, ts, offs, out):
         word_listed = keep.tile([P, HALF + P], U32, name="word_listed", align_bytes=64)
         for h in range(HALVES):
             start = P * (HALVES - 1 - h)
+            listed = word_listed[:, start : start + HALF]
             nc.vector.tensor_copy(
-                word_listed[:, start : start + HALF].rearrange("p (b j r) -> p j b r", b=BLOCKS, r=RUN),
+                listed,
                 word_pool[:].bitcast(U32).indirect(offsets[:, h * LIST_COLS : (h + 1) * LIST_COLS]),
             )
-            for b0, b1 in PARTING:
-                codes = keep.tile([P, PASSES, (b1 - b0) * P], U16, name="key_codes%d_%d" % (h, b0), align_bytes=64)
-                words = word_listed[:, start + b0 * P : start + b1 * P]
-                nc.vector.tensor_copy(codes[:], words.bitcast(U16).rearrange("p (n o) -> p o n", o=PASSES))
-                key_codes.extend(codes[:, :, i * P : (i + 1) * P] for i in range(b1 - b0))
+            halves = listed.bitcast(U16).rearrange("p (j b r o) -> p o b j r", b=BLOCKS, r=RUN, o=PASSES)
+            for (b0, b1), cuts in PARTING[h]:
+                codes = keep.tile([P, b1 - b0, PASSES, P], U16, name="key_codes%d_%d" % (h, b0), align_bytes=64)
+                by_passage = codes[:].rearrange("p b o (j r) -> p o b j r", r=RUN)
+                for j0, j1 in cuts:
+                    nc.vector.tensor_copy(by_passage[:, :, :, j0:j1, :], halves[:, :, b0:b1, j0:j1, :])
+                key_codes.extend(codes[:, i] for i in range(b1 - b0))
 
         idle = psum.tile([P, PASSES * NQ], F32, name="bank")
         for i in range(WARM):
@@ -160,11 +171,12 @@ def tile_attend_maxsim_ts_kernel(tc, qT, k_words, k_scales, ts, offs, out):
                             stop=(o == PASSES - 1),
                         )
                 factor = ts_col[:, h, b : b + 1]
-                into = best[:, b // chain, :]
-                if b % chain == 0:
-                    nc.scalar.activation(into, scores[:], COPY, scale=factor)
+                into = best[:, b % chain, :].rearrange("p (t m) -> p t m", t=QT)
+                dealt = scores[:].rearrange("p (m t) -> p t m", t=QT)
+                if b < chain:
+                    nc.scalar.activation(into, dealt, COPY, scale=factor)
                 else:
-                    nc.vector.scalar_tensor_tensor(into, scores[:], factor, into, MULT, MAX)
+                    nc.vector.scalar_tensor_tensor(into, dealt, factor, into, MULT, MAX)
         for h in range(HALVES):
             parts = BLOCKS // CHAIN[h]
             turned = psum.tile([P, BLOCKS, P], F32, name="bank")
@@ -177,4 +189,4 @@ def tile_attend_maxsim_ts_kernel(tc, qT, k_words, k_scales, ts, offs, out):
                 mybir.AxisListType.XY,
                 MAX,
             )
-        nc.sync.dma_start(out[0].rearrange("(t p) j -> p t j", p=P), result[:])
+        nc.sync.dma_start(out[0].rearrange("(p t) j -> p t j", p=P), result[:])

@@ -25,18 +25,14 @@ PASSES = 2
 PACK = 4
 HALVES = 2
 HALF = SLOTS // HALVES
-BLOCKS = HALF // P
+GROUPS = 4
+GROUP = SLOTS // GROUPS
+BLOCKS = GROUP // P
 RUN = SEG // BLOCKS
-SEGS = HALF // SEG
+SEGS = GROUP // SEG
 QT = NQ // P
 LIST_COLS = HALF // 16
-CHAIN = (2, 2)
 WARM = 2
-WHOLE = ((0, SEGS),)
-PARTING = (
-    (((0, 1), WHOLE), ((1, 4), ((0, 6), (6, 8)))),
-    (((0, 1), WHOLE), ((1, 2), WHOLE), ((2, 4), WHOLE)),
-)
 
 FLOPS = 2 * NQ * SLOTS * D
 BYTES = 4 * D * NQ + 4 * P * POOL + 32 * POOL + 4 * POOL + 2 * P * SLOTS // 16 + 4 * NQ * 16
@@ -48,6 +44,30 @@ def tile_attend_maxsim_ts_kernel(tc, qT, k_words, k_scales, ts, offs, out):
         keep = ctx.enter_context(tc.tile_pool(name="keep", bufs=1))
         psum = ctx.enter_context(tc.psum_pool(name="psum", bufs=8))
 
+        def load_queries(o):
+            raw = keep.tile([P, PACK, NQ], F32, name="q_raw%d" % o, tag="q_raw%d" % o, align_bytes=64)
+            nc.sync.dma_start(raw[:], qT[0, 512 * o : 512 * (o + 1), :].rearrange("(p j) w -> p j w", j=PACK))
+            return raw
+
+        def interleave(o, raw):
+            grouped = keep.tile([P, NQ, PACK], BF16, name="q_bf%d" % o, tag="q_bf%d" % o, align_bytes=64)
+            nc.scalar.activation(
+                grouped[:].rearrange("p (c i) j -> p c j i", i=2),
+                raw[:].rearrange("p j (c i) -> p c j i", i=2),
+                COPY,
+            )
+            return grouped
+
+        def quantise(o, grouped):
+            codes = keep.tile([P, NQ], U32, name="q_codes%d" % o, align_bytes=64)
+            scales = keep.tile([P, NQ], U8, name="q_scales%d" % o, align_bytes=64)
+            nc.vector.quantize_mx(
+                out=codes[:].bitcast(FP8X4),
+                scales=scales[:],
+                in_=grouped[:].rearrange("p w j -> p (w j)"),
+            )
+            return codes, scales
+
         offsets = keep.tile([P, SLOTS // 16], U16, name="offsets")
         nc.sync.dma_start(offsets[:], offs)
 
@@ -58,11 +78,7 @@ def tile_attend_maxsim_ts_kernel(tc, qT, k_words, k_scales, ts, offs, out):
         )
         ts_pool = keep.tile([P, POOL], F32, name="ts_pool", align_bytes=64)
         nc.sync.dma_start(ts_pool[P - 1 : P, :], ts[0:1, :])
-        q_raw = []
-        for o in range(PASSES):
-            raw = keep.tile([P, PACK, NQ], F32, name="q_raw%d" % o)
-            nc.sync.dma_start(raw[:], qT[0, 512 * o : 512 * (o + 1), :].rearrange("(p j) w -> p j w", j=PACK))
-            q_raw.append(raw)
+        q_raw0 = load_queries(0)
         word_pool = keep.tile([P, POOL], I32, name="word_pool", align_bytes=64)
         nc.sync.dma_start(word_pool[:], k_words[0].rearrange("p t b -> p (t b)").bitcast(I32))
 
@@ -80,15 +96,19 @@ def tile_attend_maxsim_ts_kernel(tc, qT, k_words, k_scales, ts, offs, out):
             planes[0][:].bitcast(I32).rearrange("p (b j w) -> p b j w", b=BLOCKS, w=RUN // 4),
             scale_listed[:].bitcast(I32).rearrange("p (j b w) -> p b j w", b=BLOCKS, w=RUN // 4),
         )
-        for po in reversed(range(PASSES)):
+
+        def place_scale_rows(o):
             for quad in range(4):
-                if po == 0 and quad == 0:
-                    continue
-                first = 16 * po + 4 * quad
-                nc.sync.dma_start(
-                    planes[po][32 * quad : 32 * quad + 4, :].bitcast(I32),
-                    planes[0][first : first + 4, :].bitcast(I32),
-                )
+                first = 16 * o + 4 * quad
+                if first:
+                    nc.sync.dma_start(
+                        planes[o][32 * quad : 32 * quad + 4, :].bitcast(I32),
+                        planes[0][first : first + 4, :].bitcast(I32),
+                    )
+
+        place_scale_rows(0)
+        q_raw1 = load_queries(1)
+        place_scale_rows(1)
 
         ts_listed = keep.tile([P, SLOTS], F32, name="ts_listed", align_bytes=64)
         nc.vector.tensor_copy(
@@ -96,97 +116,96 @@ def tile_attend_maxsim_ts_kernel(tc, qT, k_words, k_scales, ts, offs, out):
             ts_pool[:].bitcast(U32).indirect(offsets[:]),
         )
 
-        q_codes = keep.tile([P, PASSES, NQ], U32, name="q_codes", align_bytes=64)
-        q_scales = keep.tile([P, PASSES, NQ], U8, name="q_scales", align_bytes=64)
-        for o in range(PASSES):
-            grouped = keep.tile([P, NQ, PACK], BF16, name="q_bf%d" % o, align_bytes=64)
-            nc.scalar.activation(
-                grouped[:].rearrange("p (c i) j -> p c j i", i=2),
-                q_raw[o][:].rearrange("p j (c i) -> p c j i", i=2),
-                COPY,
-            )
-            nc.vector.quantize_mx(
-                out=q_codes[:, o, :].bitcast(FP8X4),
-                scales=q_scales[:, o, :],
-                in_=grouped[:].rearrange("p w j -> p (w j)"),
-            )
+        queries = [quantise(0, interleave(0, q_raw0))]
 
-        ts_col = keep.tile([P, HALVES, BLOCKS], F32, name="ts_col")
-        for h in range(HALVES):
-            turned = psum.tile([P, BLOCKS, P], F32, name="bank")
-            for b in range(BLOCKS):
-                first = (b * HALVES + h) * P
-                nc.tensor.transpose(turned[:, b, :], ts_listed[:, first : first + P], identity[:])
-            nc.scalar.copy(ts_col[:, h, :], turned[:, :, P - 1])
+        ts_col = keep.tile([P, BLOCKS, GROUPS], F32, name="ts_col")
+        for b in range(BLOCKS):
+            turned = psum.tile([P, GROUPS, P], F32, name="bank")
+            for g in range(GROUPS):
+                first = (b * GROUPS + g) * P
+                nc.tensor.transpose(turned[:, g, :], ts_listed[:, first : first + P], identity[:])
+            nc.scalar.copy(ts_col[:, b, :], turned[:, :, P - 1])
 
-        key_codes = []
-        word_listed = keep.tile([P, HALF + P], U32, name="word_listed", align_bytes=64)
-        for h in range(HALVES):
-            start = P * (HALVES - 1 - h)
+        q_bf1 = interleave(1, q_raw1)
+
+        key_codes = {}
+        word_listed = keep.tile([P, SLOTS], U32, name="word_listed", align_bytes=64)
+
+        def gather_words(h):
+            start = HALF * h
             listed = word_listed[:, start : start + HALF]
             nc.vector.tensor_copy(
                 listed,
                 word_pool[:].bitcast(U32).indirect(offsets[:, h * LIST_COLS : (h + 1) * LIST_COLS]),
             )
-            halves = listed.bitcast(U16).rearrange("p (j b r o) -> p o b j r", b=BLOCKS, r=RUN, o=PASSES)
-            for (b0, b1), cuts in PARTING[h]:
-                codes = keep.tile([P, b1 - b0, PASSES, P], U16, name="key_codes%d_%d" % (h, b0), align_bytes=64)
-                by_passage = codes[:].rearrange("p b o (j r) -> p o b j r", r=RUN)
-                for j0, j1 in cuts:
-                    nc.vector.tensor_copy(by_passage[:, :, :, j0:j1, :], halves[:, :, b0:b1, j0:j1, :])
-                key_codes.extend(codes[:, i] for i in range(b1 - b0))
+            return listed.bitcast(U16).rearrange("p (g j b r o) -> p o g b j r", j=SEGS, b=BLOCKS, r=RUN, o=PASSES)
 
-        idle = psum.tile([P, PASSES * NQ], F32, name="bank")
+        def part(pairs, h, g0, g1, o, tag):
+            codes = keep.tile([P, g1 - g0, BLOCKS, P], U16, name="key_codes%d_%d_%d" % (h, g0, o), tag=tag, align_bytes=64)
+            nc.vector.tensor_copy(codes[:].rearrange("p g b (j r) -> p g b j r", r=RUN), pairs[:, o, g0:g1])
+            for g in range(g0, g1):
+                key_codes[(2 * h + g, o)] = codes[:, g - g0]
+
+        pairs = [gather_words(h) for h in range(HALVES)]
+        for h in range(HALVES):
+            for g in range(2):
+                part(pairs[h], h, g, g + 1, 0, "k%d%d0" % (h, g))
+        part(pairs[0], 0, 0, 2, 1, "k001")
+        queries.append(quantise(1, q_bf1))
+        part(pairs[1], 1, 0, 2, 1, "q_raw1")
+
+        idle = psum.tile([P, 512], F32, name="bank")
         for i in range(WARM):
             nc.tensor.matmul_mx(
                 out=idle[:],
-                lhsT=word_pool[:, 0 : P // 2].bitcast(FP4X4),
-                lhsT_scale=scale_pool[:, 0:P],
-                rhs=q_codes[:].rearrange("p o n -> p (o n)").bitcast(FP8X4),
-                rhs_scale=q_scales[:].rearrange("p o n -> p (o n)"),
+                lhsT=queries[0][0][:, 0:P].bitcast(FP8X4),
+                lhsT_scale=queries[0][1][:, 0:P],
+                rhs=word_pool[:, 0:256].bitcast(FP4X4),
+                rhs_scale=scale_pool[:, 0:512],
                 start=True,
                 stop=True,
             )
 
-        result = keep.tile([P, QT, HALVES * SEGS], F32, name="result")
+        scores = {}
         joined = []
-        for h in range(HALVES):
-            chain = CHAIN[h]
-            best = keep.tile([P, BLOCKS // chain, NQ], F32, name="best%d" % h)
-            joined.append(best)
-            for b in range(BLOCKS):
-                first = (b * HALVES + h) * P
-                key_cols = slice(first, first + P)
-                scores = psum.tile([P, NQ], F32, name="bank")
-                for qt in range(QT):
-                    q_cols = slice(qt * P, (qt + 1) * P)
-                    for o in range(PASSES):
+        for o in range(PASSES):
+            q_codes, q_scales = queries[o]
+            for g in range(GROUPS):
+                if o == PASSES - 1:
+                    best = keep.tile([P, QT, P], F32, name="best%d" % g)
+                    joined.append(best)
+                for b in range(BLOCKS):
+                    first = (b * GROUPS + g) * P
+                    if o == 0:
+                        scores[(g, b)] = psum.tile([P, NQ], F32, name="bank")
+                    for qt in range(QT):
+                        q_cols = slice(qt * P, (qt + 1) * P)
                         nc.tensor.matmul_mx(
-                            out=scores[:, q_cols],
-                            lhsT=key_codes[h * BLOCKS + b][:, o, :].bitcast(FP4X4),
-                            lhsT_scale=planes[o][:, key_cols],
-                            rhs=q_codes[:, o, q_cols].bitcast(FP8X4),
-                            rhs_scale=q_scales[:, o, q_cols],
-                            start=(o == 0),
-                            stop=(o == PASSES - 1),
+                            out=scores[(g, b)][:, q_cols],
+                            lhsT=key_codes[(g, o)][:, b, :].bitcast(FP4X4),
+                            lhsT_scale=planes[o][:, first : first + P],
+                            rhs=q_codes[:, q_cols].bitcast(FP8X4),
+                            rhs_scale=q_scales[:, q_cols],
+                            start=(o == 0 and qt == 0),
+                            stop=(o == PASSES - 1 and qt == QT - 1),
                         )
-                factor = ts_col[:, h, b : b + 1]
-                into = best[:, b % chain, :].rearrange("p (t m) -> p t m", t=QT)
-                dealt = scores[:].rearrange("p (m t) -> p t m", t=QT)
-                if b < chain:
-                    nc.scalar.activation(into, dealt, COPY, scale=factor)
-                else:
-                    nc.vector.scalar_tensor_tensor(into, dealt, factor, into, MULT, MAX)
-        for h in range(HALVES):
-            parts = BLOCKS // CHAIN[h]
-            turned = psum.tile([P, BLOCKS, P], F32, name="bank")
-            for c in range(parts):
-                for qt in range(QT):
-                    nc.tensor.transpose(turned[:, qt * parts + c, :], joined[h][:, c, qt * P : (qt + 1) * P], identity[:])
+                    if o == PASSES - 1:
+                        factor = ts_col[:, b, g : g + 1]
+                        dealt = scores[(g, b)][:].rearrange("p (m t) -> p t m", t=QT)
+                        if b == 0:
+                            nc.scalar.activation(best[:], dealt, COPY, scale=factor)
+                        else:
+                            nc.vector.scalar_tensor_tensor(best[:], dealt, factor, best[:], MULT, MAX)
+
+        result = keep.tile([P, QT, GROUPS * SEGS], F32, name="result")
+        for g in range(GROUPS):
+            turned = psum.tile([P, QT, P], F32, name="bank")
+            for qt in range(QT):
+                nc.tensor.transpose(turned[:, qt, :], joined[g][:, qt, :], identity[:])
             nc.vector.tensor_reduce(
-                result[:, :, h * SEGS : (h + 1) * SEGS],
-                turned[:, 0 : QT * parts, :].rearrange("p (t c) (j r) -> p t j c r", c=parts, r=RUN),
-                mybir.AxisListType.XY,
+                result[:, :, g * SEGS : (g + 1) * SEGS],
+                turned[:].rearrange("p t (j r) -> p t j r", r=RUN),
+                mybir.AxisListType.X,
                 MAX,
             )
         nc.sync.dma_start(out[0].rearrange("(p t) j -> p t j", p=P), result[:])

@@ -58,8 +58,8 @@ def tile_attend_maxsim_ts_kernel(tc, qT, k_words, k_scales, ts, offs, out):
             )
             return grouped
 
-        def quantise(o, grouped):
-            codes = keep.tile([P, NQ], U32, name="q_codes%d" % o, align_bytes=64)
+        def quantise(o, grouped, tag):
+            codes = keep.tile([P, NQ], U32, name="q_codes%d" % o, tag=tag, align_bytes=64)
             scales = keep.tile([P, NQ], U8, name="q_scales%d" % o, align_bytes=64)
             nc.vector.quantize_mx(
                 out=codes[:].bitcast(FP8X4),
@@ -72,14 +72,14 @@ def tile_attend_maxsim_ts_kernel(tc, qT, k_words, k_scales, ts, offs, out):
         nc.sync.dma_start(offsets[:], offs)
 
         scale_pool = keep.tile([P, POOL], U8, name="scale_pool", align_bytes=64)
-        nc.sync.dma_start(
+        nc.scalar.dma_start(
             scale_pool[0:32, :].bitcast(I32),
             k_scales.rearrange("o f t -> (o f) t").bitcast(I32),
         )
         ts_pool = keep.tile([P, POOL], F32, name="ts_pool", align_bytes=64)
-        nc.sync.dma_start(ts_pool[P - 1 : P, :], ts[0:1, :])
+        nc.scalar.dma_start(ts_pool[P - 1 : P, :], ts[0:1, :])
         q_raw0 = load_queries(0)
-        word_pool = keep.tile([P, POOL], I32, name="word_pool", align_bytes=64)
+        word_pool = keep.tile([P, POOL], I32, name="word_pool", tag="word_pool", align_bytes=64)
         nc.sync.dma_start(word_pool[:], k_words[0].rearrange("p t b -> p (t b)").bitcast(I32))
 
         nc.vector.memset(scale_pool[32:64, :].bitcast(I32), 0)
@@ -106,8 +106,8 @@ def tile_attend_maxsim_ts_kernel(tc, qT, k_words, k_scales, ts, offs, out):
                         planes[0][first : first + 4, :].bitcast(I32),
                     )
 
-        place_scale_rows(0)
         q_raw1 = load_queries(1)
+        place_scale_rows(0)
         place_scale_rows(1)
 
         ts_listed = keep.tile([P, SLOTS], F32, name="ts_listed", align_bytes=64)
@@ -116,7 +116,7 @@ def tile_attend_maxsim_ts_kernel(tc, qT, k_words, k_scales, ts, offs, out):
             ts_pool[:].bitcast(U32).indirect(offsets[:]),
         )
 
-        queries = [quantise(0, interleave(0, q_raw0))]
+        queries = [quantise(0, interleave(0, q_raw0), "q_codes0")]
 
         ts_col = keep.tile([P, BLOCKS, GROUPS], F32, name="ts_col")
         for b in range(BLOCKS):
@@ -151,7 +151,7 @@ def tile_attend_maxsim_ts_kernel(tc, qT, k_words, k_scales, ts, offs, out):
             for g in range(2):
                 part(pairs[h], h, g, g + 1, 0, "k%d%d0" % (h, g))
         part(pairs[0], 0, 0, 2, 1, "k001")
-        queries.append(quantise(1, q_bf1))
+        queries.append(quantise(1, q_bf1, "word_pool"))
         part(pairs[1], 1, 0, 2, 1, "q_raw1")
 
         idle = psum.tile([P, 512], F32, name="bank")

@@ -68,16 +68,15 @@ def tile_attend_maxsim_ts_kernel(tc, qT, k_words, k_scales, ts, offs, out):
             )
             return codes, scales
 
-        offsets = keep.tile([P, SLOTS // 16], U16, name="offsets")
-        nc.sync.dma_start(offsets[:], offs)
-
         scale_pool = keep.tile([P, POOL], U8, name="scale_pool", align_bytes=64)
-        nc.scalar.dma_start(
+        nc.sync.dma_start(
             scale_pool[0:32, :].bitcast(I32),
             k_scales.rearrange("o f t -> (o f) t").bitcast(I32),
         )
         ts_pool = keep.tile([P, POOL], F32, name="ts_pool", align_bytes=64)
-        nc.scalar.dma_start(ts_pool[P - 1 : P, :], ts[0:1, :])
+        nc.sync.dma_start(ts_pool[P - 1 : P, :], ts[0:1, :])
+        offsets = keep.tile([P, SLOTS // 16], U16, name="offsets")
+        nc.sync.dma_start(offsets[:], offs)
         q_raw0 = load_queries(0)
         word_pool = keep.tile([P, POOL], I32, name="word_pool", tag="word_pool", align_bytes=64)
         nc.sync.dma_start(word_pool[:], k_words[0].rearrange("p t b -> p (t b)").bitcast(I32))

@@ -16,26 +16,40 @@ MULT = mybir.AluOpType.mult
 MAX = mybir.AluOpType.max
 
 P = 128
+QUADRANT = 32
 POOL = 4096
 SLOTS = 1024
 D = 1024
 NQ = 256
-SEG = 64
-PASSES = 2
+PASSAGE = 64
 PACK = 4
+K_PASS = P * PACK
+PASSES = D // K_PASS
+SCALE_ROWS = K_PASS // 32
+QUAD_ROWS = SCALE_ROWS * QUADRANT // P
 HALVES = 2
 HALF = SLOTS // HALVES
+HALF_COLS = HALF // 16
 GROUPS = 4
-GROUP = SLOTS // GROUPS
-BLOCKS = GROUP // P
-RUN = SEG // BLOCKS
-SEGS = GROUP // SEG
+HALF_GROUPS = GROUPS // HALVES
+BLOCKS = SLOTS // GROUPS // P
+RUN = PASSAGE // BLOCKS
+GROUP_PASSAGES = P // RUN
 QT = NQ // P
-LIST_COLS = HALF // 16
-WARM = 2
+BANK = 512
+WARM_UP_PASSES = 2
+ALL_QUERIES = (slice(0, NQ),)
+BY_QUERY_TILE = tuple(slice(t * P, (t + 1) * P) for t in range(QT))
 
 FLOPS = 2 * NQ * SLOTS * D
-BYTES = 4 * D * NQ + 4 * P * POOL + 32 * POOL + 4 * POOL + 2 * P * SLOTS // 16 + 4 * NQ * 16
+BYTES = (
+    4 * D * NQ
+    + 4 * P * POOL
+    + PASSES * SCALE_ROWS * POOL
+    + 4 * POOL
+    + 2 * P * SLOTS // 16
+    + 4 * NQ * SLOTS // PASSAGE
+)
 
 
 def tile_attend_maxsim_ts_kernel(tc, qT, k_words, k_scales, ts, offs, out):
@@ -46,31 +60,35 @@ def tile_attend_maxsim_ts_kernel(tc, qT, k_words, k_scales, ts, offs, out):
 
         def load_queries(o):
             raw = keep.tile([P, PACK, NQ], F32, name="q_raw%d" % o, tag="q_raw%d" % o, align_bytes=64)
-            nc.sync.dma_start(raw[:], qT[0, 512 * o : 512 * (o + 1), :].rearrange("(p j) w -> p j w", j=PACK))
+            nc.sync.dma_start(
+                raw[:], qT[0, K_PASS * o : K_PASS * (o + 1), :].rearrange("(p j) w -> p j w", j=PACK)
+            )
             return raw
 
-        def interleave(o, raw):
+        def interleave(o, raw, pieces):
             grouped = keep.tile([P, NQ, PACK], BF16, name="q_bf%d" % o, tag="q_bf%d" % o, align_bytes=64)
-            nc.scalar.activation(
-                grouped[:].rearrange("p (c i) j -> p c j i", i=2),
-                raw[:].rearrange("p j (c i) -> p c j i", i=2),
-                COPY,
-            )
+            for cols in pieces:
+                nc.scalar.activation(
+                    grouped[:, cols, :].rearrange("p (c i) j -> p c j i", i=2),
+                    raw[:, :, cols].rearrange("p j (c i) -> p c j i", i=2),
+                    COPY,
+                )
             return grouped
 
-        def quantise(o, grouped, tag):
+        def quantise(o, grouped, tag, pieces):
             codes = keep.tile([P, NQ], U32, name="q_codes%d" % o, tag=tag, align_bytes=64)
             scales = keep.tile([P, NQ], U8, name="q_scales%d" % o, align_bytes=64)
-            nc.vector.quantize_mx(
-                out=codes[:].bitcast(FP8X4),
-                scales=scales[:],
-                in_=grouped[:].rearrange("p w j -> p (w j)"),
-            )
+            for cols in pieces:
+                nc.vector.quantize_mx(
+                    out=codes[:, cols].bitcast(FP8X4),
+                    scales=scales[:, cols],
+                    in_=grouped[:, cols, :].rearrange("p w j -> p (w j)"),
+                )
             return codes, scales
 
         scale_pool = keep.tile([P, POOL], U8, name="scale_pool", align_bytes=64)
         nc.sync.dma_start(
-            scale_pool[0:32, :].bitcast(I32),
+            scale_pool[0:QUADRANT, :].bitcast(I32),
             k_scales.rearrange("o f t -> (o f) t").bitcast(I32),
         )
         ts_pool = keep.tile([P, POOL], F32, name="ts_pool", align_bytes=64)
@@ -81,8 +99,8 @@ def tile_attend_maxsim_ts_kernel(tc, qT, k_words, k_scales, ts, offs, out):
         word_pool = keep.tile([P, POOL], I32, name="word_pool", tag="word_pool", align_bytes=64)
         nc.sync.dma_start(word_pool[:], k_words[0].rearrange("p t b -> p (t b)").bitcast(I32))
 
-        nc.vector.memset(scale_pool[32:64, :].bitcast(I32), 0)
-        nc.vector.memset(scale_pool[64:128, :].bitcast(I32), 0)
+        nc.vector.memset(scale_pool[QUADRANT : 2 * QUADRANT, :].bitcast(I32), 0)
+        nc.vector.memset(scale_pool[2 * QUADRANT : P, :].bitcast(I32), 0)
         nc.vector.memset(ts_pool[0 : P - 1, :], 0.0)
         identity = keep.tile([P, P], F32, name="identity")
         make_identity(nc, identity[:])
@@ -97,12 +115,12 @@ def tile_attend_maxsim_ts_kernel(tc, qT, k_words, k_scales, ts, offs, out):
         )
 
         def place_scale_rows(o):
-            for quad in range(4):
-                first = 16 * o + 4 * quad
+            for quad in range(P // QUADRANT):
+                first = SCALE_ROWS * o + QUAD_ROWS * quad
                 if first:
                     nc.sync.dma_start(
-                        planes[o][32 * quad : 32 * quad + 4, :].bitcast(I32),
-                        planes[0][first : first + 4, :].bitcast(I32),
+                        planes[o][QUADRANT * quad : QUADRANT * quad + QUAD_ROWS, :].bitcast(I32),
+                        planes[0][first : first + QUAD_ROWS, :].bitcast(I32),
                     )
 
         q_raw1 = load_queries(1)
@@ -115,7 +133,7 @@ def tile_attend_maxsim_ts_kernel(tc, qT, k_words, k_scales, ts, offs, out):
             ts_pool[:].bitcast(U32).indirect(offsets[:]),
         )
 
-        queries = [quantise(0, interleave(0, q_raw0), "q_codes0")]
+        queries = [quantise(0, interleave(0, q_raw0, ALL_QUERIES), "q_codes0", ALL_QUERIES)]
 
         ts_col = keep.tile([P, BLOCKS, GROUPS], F32, name="ts_col")
         for b in range(BLOCKS):
@@ -125,42 +143,45 @@ def tile_attend_maxsim_ts_kernel(tc, qT, k_words, k_scales, ts, offs, out):
                 nc.tensor.transpose(turned[:, g, :], ts_listed[:, first : first + P], identity[:])
             nc.scalar.copy(ts_col[:, b, :], turned[:, :, P - 1])
 
-        q_bf1 = interleave(1, q_raw1)
+        q_bf1 = interleave(1, q_raw1, BY_QUERY_TILE)
 
         key_codes = {}
         word_listed = keep.tile([P, SLOTS], U32, name="word_listed", align_bytes=64)
 
         def gather_words(h):
-            start = HALF * h
-            listed = word_listed[:, start : start + HALF]
+            listed = word_listed[:, HALF * h : HALF * (h + 1)]
             nc.vector.tensor_copy(
                 listed,
-                word_pool[:].bitcast(U32).indirect(offsets[:, h * LIST_COLS : (h + 1) * LIST_COLS]),
+                word_pool[:].bitcast(U32).indirect(offsets[:, h * HALF_COLS : (h + 1) * HALF_COLS]),
             )
-            return listed.bitcast(U16).rearrange("p (g j b r o) -> p o g b j r", j=SEGS, b=BLOCKS, r=RUN, o=PASSES)
+            return listed.bitcast(U16).rearrange(
+                "p (g j b r o) -> p o g b j r", j=GROUP_PASSAGES, b=BLOCKS, r=RUN, o=PASSES
+            )
 
         def part(pairs, h, g0, g1, o, tag):
-            codes = keep.tile([P, g1 - g0, BLOCKS, P], U16, name="key_codes%d_%d_%d" % (h, g0, o), tag=tag, align_bytes=64)
+            codes = keep.tile(
+                [P, g1 - g0, BLOCKS, P], U16, name="key_codes%d_%d_%d" % (h, g0, o), tag=tag, align_bytes=64
+            )
             nc.vector.tensor_copy(codes[:].rearrange("p g b (j r) -> p g b j r", r=RUN), pairs[:, o, g0:g1])
             for g in range(g0, g1):
-                key_codes[(2 * h + g, o)] = codes[:, g - g0]
+                key_codes[(HALF_GROUPS * h + g, o)] = codes[:, g - g0]
 
         pairs = [gather_words(h) for h in range(HALVES)]
         for h in range(HALVES):
-            for g in range(2):
+            for g in range(HALF_GROUPS):
                 part(pairs[h], h, g, g + 1, 0, "k%d%d0" % (h, g))
-        part(pairs[0], 0, 0, 2, 1, "k001")
-        queries.append(quantise(1, q_bf1, "word_pool"))
-        part(pairs[1], 1, 0, 2, 1, "q_raw1")
+        part(pairs[0], 0, 0, HALF_GROUPS, 1, "k001")
+        queries.append(quantise(1, q_bf1, "word_pool", BY_QUERY_TILE))
+        part(pairs[1], 1, 0, HALF_GROUPS, 1, "q_raw1")
 
-        idle = psum.tile([P, 512], F32, name="bank")
-        for i in range(WARM):
+        idle = psum.tile([P, BANK], F32, name="bank")
+        for i in range(WARM_UP_PASSES):
             nc.tensor.matmul_mx(
                 out=idle[:],
                 lhsT=queries[0][0][:, 0:P].bitcast(FP8X4),
                 lhsT_scale=queries[0][1][:, 0:P],
-                rhs=word_pool[:, 0:256].bitcast(FP4X4),
-                rhs_scale=scale_pool[:, 0:512],
+                rhs=word_pool[:, 0 : BANK // PASSES].bitcast(FP4X4),
+                rhs_scale=scale_pool[:, 0:BANK],
                 start=True,
                 stop=True,
             )
@@ -196,13 +217,13 @@ def tile_attend_maxsim_ts_kernel(tc, qT, k_words, k_scales, ts, offs, out):
                         else:
                             nc.vector.scalar_tensor_tensor(best[:], dealt, factor, best[:], MULT, MAX)
 
-        result = keep.tile([P, QT, GROUPS * SEGS], F32, name="result")
+        result = keep.tile([P, QT, GROUPS * GROUP_PASSAGES], F32, name="result")
         for g in range(GROUPS):
             turned = psum.tile([P, QT, P], F32, name="bank")
-            for qt in range(QT):
-                nc.tensor.transpose(turned[:, qt, :], joined[g][:, qt, :], identity[:])
+            for t in range(QT):
+                nc.tensor.transpose(turned[:, t, :], joined[g][:, t, :], identity[:])
             nc.vector.tensor_reduce(
-                result[:, :, g * SEGS : (g + 1) * SEGS],
+                result[:, :, g * GROUP_PASSAGES : (g + 1) * GROUP_PASSAGES],
                 turned[:].rearrange("p t (j r) -> p t j r", r=RUN),
                 mybir.AxisListType.X,
                 MAX,

@@ -36,8 +36,6 @@ BLOCKS = SLOTS // GROUPS // P
 RUN = PASSAGE // BLOCKS
 GROUP_PASSAGES = P // RUN
 QT = NQ // P
-BANK = 512
-WARM_UP_PASSES = 2
 ALL_QUERIES = (slice(0, NQ),)
 BY_QUERY_TILE = tuple(slice(t * P, (t + 1) * P) for t in range(QT))
 
@@ -174,18 +172,6 @@ def tile_attend_maxsim_ts_kernel(tc, qT, k_words, k_scales, ts, offs, out):
         queries.append(quantise(1, q_bf1, "word_pool", BY_QUERY_TILE))
         part(pairs[1], 1, 0, HALF_GROUPS, 1, "q_raw1")
 
-        idle = psum.tile([P, BANK], F32, name="bank")
-        for i in range(WARM_UP_PASSES):
-            nc.tensor.matmul_mx(
-                out=idle[:],
-                lhsT=queries[0][0][:, 0:P].bitcast(FP8X4),
-                lhsT_scale=queries[0][1][:, 0:P],
-                rhs=word_pool[:, 0 : BANK // PASSES].bitcast(FP4X4),
-                rhs_scale=scale_pool[:, 0:BANK],
-                start=True,
-                stop=True,
-            )
-
         scores = {}
         joined = []
         for o in range(PASSES):
@@ -198,17 +184,15 @@ def tile_attend_maxsim_ts_kernel(tc, qT, k_words, k_scales, ts, offs, out):
                     first = (b * GROUPS + g) * P
                     if o == 0:
                         scores[(g, b)] = psum.tile([P, NQ], F32, name="bank")
-                    for qt in range(QT):
-                        q_cols = slice(qt * P, (qt + 1) * P)
-                        nc.tensor.matmul_mx(
-                            out=scores[(g, b)][:, q_cols],
-                            lhsT=key_codes[(g, o)][:, b, :].bitcast(FP4X4),
-                            lhsT_scale=planes[o][:, first : first + P],
-                            rhs=q_codes[:, q_cols].bitcast(FP8X4),
-                            rhs_scale=q_scales[:, q_cols],
-                            start=(o == 0 and qt == 0),
-                            stop=(o == PASSES - 1 and qt == QT - 1),
-                        )
+                    nc.tensor.matmul_mx(
+                        out=scores[(g, b)][:],
+                        lhsT=key_codes[(g, o)][:, b, :].bitcast(FP4X4),
+                        lhsT_scale=planes[o][:, first : first + P],
+                        rhs=q_codes[:].bitcast(FP8X4),
+                        rhs_scale=q_scales[:],
+                        start=(o == 0),
+                        stop=(o == PASSES - 1),
+                    )
                     if o == PASSES - 1:
                         factor = ts_col[:, b, g : g + 1]
                         dealt = scores[(g, b)][:].rearrange("p (m t) -> p t m", t=QT)

@@ -1,7 +1,6 @@
 from contextlib import ExitStack
 
 import concourse.mybir as mybir
-from concourse.masks import make_identity
 
 F32 = mybir.dt.float32
 BF16 = mybir.dt.bfloat16
@@ -35,7 +34,12 @@ HALF_GROUPS = GROUPS // HALVES
 BLOCKS = SLOTS // GROUPS // P
 RUN = PASSAGE // BLOCKS
 GROUP_PASSAGES = P // RUN
+HALF_BLOCKS = HALF // P
+SHARING = (4, 2)
+GROUP = SLOTS // GROUPS
 QT = NQ // P
+RAW_BYTES = 4 * PACK * NQ
+KEY_BYTES = 2 * HALF
 ALL_QUERIES = (slice(0, NQ),)
 BY_QUERY_TILE = tuple(slice(t * P, (t + 1) * P) for t in range(QT))
 
@@ -54,24 +58,21 @@ def tile_attend_maxsim_ts_kernel(tc, qT, k_words, k_scales, ts, offs, out):
     nc = tc.nc
     with ExitStack() as ctx:
         keep = ctx.enter_context(tc.tile_pool(name="keep", bufs=1))
-        psum = ctx.enter_context(tc.psum_pool(name="psum", bufs=8))
+        reuse = ctx.enter_context(tc.tile_pool(name="reuse", bufs=1))
+        sums = ctx.enter_context(tc.psum_pool(name="sums", bufs=1))
 
         def load_queries(o):
-            raw = keep.tile([P, PACK, NQ], F32, name="q_raw%d" % o, tag="q_raw%d" % o, align_bytes=64)
+            raw = reuse.tile([P, PACK, NQ], F32, name="q_raw%d" % o, align_bytes=64, offset=RAW_BYTES * o)
             nc.sync.dma_start(
                 raw[:], qT[0, K_PASS * o : K_PASS * (o + 1), :].rearrange("(p j) w -> p j w", j=PACK)
             )
             return raw
 
-        def interleave(o, raw, pieces):
-            grouped = keep.tile([P, NQ, PACK], BF16, name="q_bf%d" % o, tag="q_bf%d" % o, align_bytes=64)
-            for cols in pieces:
-                nc.scalar.activation(
-                    grouped[:, cols, :].rearrange("p (c i) j -> p c j i", i=2),
-                    raw[:, :, cols].rearrange("p j (c i) -> p c j i", i=2),
-                    COPY,
-                )
-            return grouped
+        def paired(grouped, raw, cols):
+            return (
+                grouped[:, cols, :].rearrange("p (c i) j -> p c j i", i=2),
+                raw[:, :, cols].rearrange("p j (c i) -> p c j i", i=2),
+            )
 
         def quantise(o, grouped, tag, pieces):
             codes = keep.tile([P, NQ], U32, name="q_codes%d" % o, tag=tag, align_bytes=64)
@@ -93,24 +94,35 @@ def tile_attend_maxsim_ts_kernel(tc, qT, k_words, k_scales, ts, offs, out):
         nc.sync.dma_start(ts_pool[P - 1 : P, :], ts[0:1, :])
         offsets = keep.tile([P, SLOTS // 16], U16, name="offsets")
         nc.sync.dma_start(offsets[:], offs)
-        q_raw0 = load_queries(0)
+        q_raw = [load_queries(0)]
         word_pool = keep.tile([P, POOL], I32, name="word_pool", tag="word_pool", align_bytes=64)
         nc.sync.dma_start(word_pool[:], k_words[0].rearrange("p t b -> p (t b)").bitcast(I32))
 
         nc.vector.memset(scale_pool[QUADRANT : 2 * QUADRANT, :].bitcast(I32), 0)
         nc.vector.memset(scale_pool[2 * QUADRANT : P, :].bitcast(I32), 0)
         nc.vector.memset(ts_pool[0 : P - 1, :], 0.0)
-        identity = keep.tile([P, P], F32, name="identity")
-        make_identity(nc, identity[:])
+        planes = [keep.tile([P, SLOTS], U8, name="plane%d" % o, align_bytes=64) for o in range(PASSES)]
 
         scale_listed = keep.tile([P, SLOTS], U8, name="scale_listed", align_bytes=64)
         nc.vector.tensor_copy(scale_listed[:], scale_pool[:].indirect(offsets[:]))
-        planes = [keep.tile([P, SLOTS], U8, name="plane%d" % o, align_bytes=64) for o in range(PASSES)]
         nc.vector.memset(planes[1][:].bitcast(I32), 0)
-        nc.vector.tensor_copy(
-            planes[0][:].bitcast(I32).rearrange("p (b j w) -> p b j w", b=BLOCKS, w=RUN // 4),
-            scale_listed[:].bitcast(I32).rearrange("p (j b w) -> p b j w", b=BLOCKS, w=RUN // 4),
-        )
+        distance = keep.tile([P, P], I32, name="distance")
+        nc.gpsimd.iota(distance[:], [[-1, P]], base=0, channel_multiplier=1)
+        identity = keep.tile([P, P], F32, name="identity")
+        nc.vector.tensor_scalar(identity[:], distance[:], 0, None, mybir.AluOpType.is_equal)
+
+
+        def block_order(dst, src, h, per_slot):
+            blocks = SHARING[h]
+            run = PASSAGE // blocks // per_slot
+            cols = slice(h * HALF // per_slot, (h + 1) * HALF // per_slot)
+            return (
+                dst[:, cols].rearrange("p (g b j r) -> p g b j r", b=blocks, j=P * blocks // PASSAGE, r=run),
+                src[:, cols].rearrange("p (g j b r) -> p g b j r", b=blocks, j=P * blocks // PASSAGE, r=run),
+            )
+
+        for h in range(HALVES):
+            nc.vector.tensor_copy(*block_order(planes[0][:].bitcast(I32), scale_listed[:].bitcast(I32), h, 4))
 
         def place_scale_rows(o):
             for quad in range(P // QUADRANT):
@@ -121,94 +133,113 @@ def tile_attend_maxsim_ts_kernel(tc, qT, k_words, k_scales, ts, offs, out):
                         planes[0][first : first + QUAD_ROWS, :].bitcast(I32),
                     )
 
-        q_raw1 = load_queries(1)
+        q_raw.append(load_queries(1))
         place_scale_rows(0)
         place_scale_rows(1)
 
-        ts_listed = keep.tile([P, SLOTS], F32, name="ts_listed", align_bytes=64)
+        ts_blocks = [keep.tile([P, HALF], F32, name="ts_blocks%d" % h, align_bytes=64) for h in range(HALVES)]
         nc.vector.tensor_copy(
-            ts_listed[:].bitcast(U32).rearrange("p (b j r) -> p j b r", b=BLOCKS, r=RUN),
-            ts_pool[:].bitcast(U32).indirect(offsets[:]),
+            ts_blocks[0][:].bitcast(U32).rearrange("p (b j r) -> p j b r", b=HALF_BLOCKS, r=PASSAGE // HALF_BLOCKS),
+            ts_pool[:].bitcast(U32).indirect(offsets[:, 0:HALF_COLS]),
         )
 
-        queries = [quantise(0, interleave(0, q_raw0, ALL_QUERIES), "q_codes0", ALL_QUERIES)]
+        q_bf = [keep.tile([P, NQ, PACK], BF16, name="q_bf%d" % o, align_bytes=64) for o in range(PASSES)]
+        nc.scalar.activation(*paired(q_bf[0], q_raw[0], ALL_QUERIES[0]), COPY)
+        queries = [quantise(0, q_bf[0], "q_codes0", ALL_QUERIES)]
 
-        ts_col = keep.tile([P, BLOCKS, GROUPS], F32, name="ts_col")
-        for b in range(BLOCKS):
-            turned = psum.tile([P, GROUPS, P], F32, name="bank")
-            for g in range(GROUPS):
-                first = (b * GROUPS + g) * P
-                nc.tensor.transpose(turned[:, g, :], ts_listed[:, first : first + P], identity[:])
-            nc.scalar.copy(ts_col[:, b, :], turned[:, :, P - 1])
+        ts_listed = reuse.tile([P, HALF], F32, name="ts_listed", align_bytes=64, offset=0)
+        nc.scalar.activation(ts_listed[:], ts_pool[:].indirect(offsets[:, HALF_COLS : 2 * HALF_COLS]), COPY)
+        nc.scalar.copy(
+            ts_blocks[1][:].rearrange("p (g b j r) -> p g b j r", g=HALF_GROUPS, b=BLOCKS, r=RUN),
+            ts_listed[:].rearrange("p (g j b r) -> p g b j r", g=HALF_GROUPS, b=BLOCKS, r=RUN),
+        )
 
-        q_bf1 = interleave(1, q_raw1, BY_QUERY_TILE)
+        ts_col = reuse.tile([P, HALVES, HALF_BLOCKS], F32, name="ts_col", align_bytes=64, offset=0)
+        for h in range(HALVES):
+            turned = sums.tile([P, HALF_BLOCKS, P], F32, name="sum%d" % (1 - h))
+            for k in range(HALF_BLOCKS):
+                nc.tensor.transpose(turned[:, k, :], ts_blocks[h][:, k * P : (k + 1) * P], identity[:])
+            nc.scalar.copy(ts_col[:, h, :], turned[:, :, P - 1])
+
+        nc.scalar.activation(*paired(q_bf[1], q_raw[1], ALL_QUERIES[0]), COPY)
 
         key_codes = {}
-        word_listed = keep.tile([P, SLOTS], U32, name="word_listed", align_bytes=64)
 
-        def gather_words(h):
-            listed = word_listed[:, HALF * h : HALF * (h + 1)]
+        def gather_words(name, first, slots, blocks, pool, offset):
+            listed = pool.tile([P, slots], U32, name=name, align_bytes=64, offset=offset)
             nc.vector.tensor_copy(
-                listed,
-                word_pool[:].bitcast(U32).indirect(offsets[:, h * HALF_COLS : (h + 1) * HALF_COLS]),
+                listed[:],
+                word_pool[:].bitcast(U32).indirect(offsets[:, first // 16 : (first + slots) // 16]),
             )
-            return listed.bitcast(U16).rearrange(
-                "p (g j b r o) -> p o g b j r", j=GROUP_PASSAGES, b=BLOCKS, r=RUN, o=PASSES
+            return listed[:].bitcast(U16).rearrange(
+                "p (j b r o) -> p o b j r", b=blocks, r=PASSAGE // blocks, o=PASSES
             )
 
-        def part(pairs, h, g0, g1, o, tag):
-            codes = keep.tile(
-                [P, g1 - g0, BLOCKS, P], U16, name="key_codes%d_%d_%d" % (h, g0, o), tag=tag, align_bytes=64
-            )
-            nc.vector.tensor_copy(codes[:].rearrange("p g b (j r) -> p g b j r", r=RUN), pairs[:, o, g0:g1])
-            for g in range(g0, g1):
-                key_codes[(HALF_GROUPS * h + g, o)] = codes[:, g - g0]
+        def part(name, words, first, passes, pool, offset):
+            blocks, run = words.shape[2], words.shape[4]
+            codes = pool.tile([P, len(passes), blocks, P], U16, name=name, align_bytes=64, offset=offset)
+            nc.vector.tensor_copy(codes[:].rearrange("p o b (j r) -> p o b j r", r=run), words)
+            for i, o in enumerate(passes):
+                for b in range(blocks):
+                    key_codes[(first + b, o)] = codes[:, i, b, :]
 
-        pairs = [gather_words(h) for h in range(HALVES)]
-        for h in range(HALVES):
-            for g in range(HALF_GROUPS):
-                part(pairs[h], h, g, g + 1, 0, "k%d%d0" % (h, g))
-        part(pairs[0], 0, 0, HALF_GROUPS, 1, "k001")
-        queries.append(quantise(1, q_bf1, "word_pool", BY_QUERY_TILE))
-        part(pairs[1], 1, 0, HALF_GROUPS, 1, "q_raw1")
+        words0 = gather_words("words0", 0, HALF, HALF_BLOCKS, keep, None)
+        words2 = gather_words("words2", HALF, GROUP, BLOCKS, keep, None)
+        part("keys00", words0[:, 0:1, 0:BLOCKS], 0, (0,), keep, None)
+        part("keys01", words0[:, 0:1, BLOCKS:HALF_BLOCKS], BLOCKS, (0,), keep, None)
+        part("keys1", words0[:, 1:2], 0, (1,), keep, None)
+        queries.append(quantise(1, q_bf[1], "q_codes1", ALL_QUERIES))
+        words3 = gather_words("words3", HALF + GROUP, GROUP, BLOCKS, reuse, RAW_BYTES)
+        part("keys2", words2, HALF_BLOCKS, (0, 1), reuse, RAW_BYTES + KEY_BYTES)
+        part("keys3", words3, HALF_BLOCKS + BLOCKS, (0, 1), keep, None)
 
         scores = {}
-        joined = []
-        for o in range(PASSES):
+        joined = {}
+
+        def multiply(g, b, o, cols, start, stop):
             q_codes, q_scales = queries[o]
-            for g in range(GROUPS):
-                if o == PASSES - 1:
-                    best = keep.tile([P, QT, P], F32, name="best%d" % g)
-                    joined.append(best)
-                for b in range(BLOCKS):
-                    first = (b * GROUPS + g) * P
-                    if o == 0:
-                        scores[(g, b)] = psum.tile([P, NQ], F32, name="bank")
-                    nc.tensor.matmul_mx(
-                        out=scores[(g, b)][:],
-                        lhsT=key_codes[(g, o)][:, b, :].bitcast(FP4X4),
-                        lhsT_scale=planes[o][:, first : first + P],
-                        rhs=q_codes[:].bitcast(FP8X4),
-                        rhs_scale=q_scales[:],
-                        start=(o == 0),
-                        stop=(o == PASSES - 1),
-                    )
-                    if o == PASSES - 1:
-                        factor = ts_col[:, b, g : g + 1]
-                        dealt = scores[(g, b)][:].rearrange("p (m t) -> p t m", t=QT)
-                        if b == 0:
-                            nc.scalar.activation(best[:], dealt, COPY, scale=factor)
-                        else:
-                            nc.vector.scalar_tensor_tensor(best[:], dealt, factor, best[:], MULT, MAX)
+            n = BLOCKS * g + b
+            first = n * P
+            if start:
+                scores[(g, b)] = sums.tile([P, NQ], F32, name="sum%d" % n)
+            nc.tensor.matmul_mx(
+                out=scores[(g, b)][:, cols],
+                lhsT=key_codes[(n, o)].bitcast(FP4X4),
+                lhsT_scale=planes[o][:, first : first + P],
+                rhs=q_codes[:, cols].bitcast(FP8X4),
+                rhs_scale=q_scales[:, cols],
+                start=start,
+                stop=stop,
+            )
+            if stop:
+                factor = ts_col[:, n // HALF_BLOCKS, n % HALF_BLOCKS : n % HALF_BLOCKS + 1]
+                dealt = scores[(g, b)][:].rearrange("p (m t) -> p t m", t=QT)
+                if b == 0:
+                    joined[g] = keep.tile([P, QT, P], F32, name="best%d" % g)
+                    nc.scalar.activation(joined[g][:], dealt, COPY, scale=factor)
+                else:
+                    nc.vector.scalar_tensor_tensor(joined[g][:], dealt, factor, joined[g][:], MULT, MAX)
+
+        for g in range(HALF_GROUPS):
+            for b in range(BLOCKS):
+                multiply(g, b, 0, ALL_QUERIES[0], True, False)
+        for b in range(BLOCKS):
+            for g in range(HALF_GROUPS):
+                multiply(g, b, 1, ALL_QUERIES[0], False, True)
+        nc.vector.tensor_tensor(joined[1][:], joined[0][:], joined[1][:], MAX)
+        for g in range(HALF_GROUPS, GROUPS):
+            for b in range(BLOCKS):
+                multiply(g, b, 1, ALL_QUERIES[0], True, False)
+                multiply(g, b, 0, ALL_QUERIES[0], False, True)
 
         result = keep.tile([P, QT, GROUPS * GROUP_PASSAGES], F32, name="result")
-        for g in range(GROUPS):
-            turned = psum.tile([P, QT, P], F32, name="bank")
+        for g, first, run in ((1, 0, 16), (2, 8, 32), (3, 12, 32)):
+            turned = sums.tile([P, QT, P], F32, name="sum%d" % (4 if g == 1 else 6 if g == 2 else 7))
             for t in range(QT):
                 nc.tensor.transpose(turned[:, t, :], joined[g][:, t, :], identity[:])
             nc.vector.tensor_reduce(
-                result[:, :, g * GROUP_PASSAGES : (g + 1) * GROUP_PASSAGES],
-                turned[:].rearrange("p t (j r) -> p t j r", r=RUN),
+                result[:, :, first : first + P // run],
+                turned[:].rearrange("p t (j r) -> p t j r", r=run),
                 mybir.AxisListType.X,
                 MAX,
             )

@@ -138,25 +138,22 @@ def tile_attend_maxsim_ts_kernel(tc, qT, k_words, k_scales, ts, offs, out):
         place_scale_rows(1)
 
         ts_blocks = [keep.tile([P, HALF], F32, name="ts_blocks%d" % h, align_bytes=64) for h in range(HALVES)]
-        nc.vector.tensor_copy(
-            ts_blocks[0][:].bitcast(U32).rearrange("p (b j r) -> p j b r", b=HALF_BLOCKS, r=PASSAGE // HALF_BLOCKS),
-            ts_pool[:].bitcast(U32).indirect(offsets[:, 0:HALF_COLS]),
-        )
+        for h in range(HALVES):
+            blocks = SHARING[h]
+            nc.vector.tensor_copy(
+                ts_blocks[h][:]
+                .bitcast(U32)
+                .rearrange("p (g b j r) -> p g j b r", b=blocks, j=P * blocks // PASSAGE, r=PASSAGE // blocks),
+                ts_pool[:].bitcast(U32).indirect(offsets[:, h * HALF_COLS : (h + 1) * HALF_COLS]),
+            )
 
         q_bf = [keep.tile([P, NQ, PACK], BF16, name="q_bf%d" % o, align_bytes=64) for o in range(PASSES)]
         nc.scalar.activation(*paired(q_bf[0], q_raw[0], ALL_QUERIES[0]), COPY)
         queries = [quantise(0, q_bf[0], "q_codes0", ALL_QUERIES)]
 
-        ts_listed = reuse.tile([P, HALF], F32, name="ts_listed", align_bytes=64, offset=0)
-        nc.scalar.activation(ts_listed[:], ts_pool[:].indirect(offsets[:, HALF_COLS : 2 * HALF_COLS]), COPY)
-        nc.scalar.copy(
-            ts_blocks[1][:].rearrange("p (g b j r) -> p g b j r", g=HALF_GROUPS, b=BLOCKS, r=RUN),
-            ts_listed[:].rearrange("p (g j b r) -> p g b j r", g=HALF_GROUPS, b=BLOCKS, r=RUN),
-        )
-
-        ts_col = reuse.tile([P, HALVES, HALF_BLOCKS], F32, name="ts_col", align_bytes=64, offset=0)
+        ts_col = keep.tile([P, HALVES, HALF_BLOCKS], F32, name="ts_col")
         for h in range(HALVES):
-            turned = sums.tile([P, HALF_BLOCKS, P], F32, name="sum%d" % (1 - h))
+            turned = sums.tile([P, HALF_BLOCKS, P], F32, name="sum%d" % (6 + h))
             for k in range(HALF_BLOCKS):
                 nc.tensor.transpose(turned[:, k, :], ts_blocks[h][:, k * P : (k + 1) * P], identity[:])
             nc.scalar.copy(ts_col[:, h, :], turned[:, :, P - 1])

@@ -128,7 +128,8 @@ def tile_attend_maxsim_ts_kernel(tc, qT, k_words, k_scales, ts, offs, out):
             for quad in range(P // QUADRANT):
                 first = SCALE_ROWS * o + QUAD_ROWS * quad
                 if first:
-                    nc.sync.dma_start(
+                    queue = nc.gpsimd if first == PASSES * SCALE_ROWS - QUAD_ROWS else nc.sync
+                    queue.dma_start(
                         planes[o][QUADRANT * quad : QUADRANT * quad + QUAD_ROWS, :].bitcast(I32),
                         planes[0][first : first + QUAD_ROWS, :].bitcast(I32),
                     )
@@ -158,7 +159,7 @@ def tile_attend_maxsim_ts_kernel(tc, qT, k_words, k_scales, ts, offs, out):
                 nc.tensor.transpose(turned[:, k, :], ts_blocks[h][:, k * P : (k + 1) * P], identity[:])
             nc.scalar.copy(ts_col[:, h, :], turned[:, :, P - 1])
 
-        nc.scalar.activation(*paired(q_bf[1], q_raw[1], ALL_QUERIES[0]), COPY)
+        nc.scalar.activation(*paired(q_bf[1], q_raw[1], BY_QUERY_TILE[1]), COPY)
 
         key_codes = {}
 
@@ -185,9 +186,10 @@ def tile_attend_maxsim_ts_kernel(tc, qT, k_words, k_scales, ts, offs, out):
         part("keys00", words0[:, 0:1, 0:BLOCKS], 0, (0,), keep, None)
         part("keys01", words0[:, 0:1, BLOCKS:HALF_BLOCKS], BLOCKS, (0,), keep, None)
         part("keys1", words0[:, 1:2], 0, (1,), keep, None)
+        nc.vector.tensor_copy(*paired(q_bf[1], q_raw[1], BY_QUERY_TILE[0]))
+        part("keys2", words2, HALF_BLOCKS, (0, 1), reuse, RAW_BYTES + KEY_BYTES)
         queries.append(quantise(1, q_bf[1], "q_codes1", ALL_QUERIES))
         words3 = gather_words("words3", HALF + GROUP, GROUP, BLOCKS, reuse, RAW_BYTES)
-        part("keys2", words2, HALF_BLOCKS, (0, 1), reuse, RAW_BYTES + KEY_BYTES)
         part("keys3", words3, HALF_BLOCKS + BLOCKS, (0, 1), keep, None)
 
         scores = {}
@@ -220,14 +222,18 @@ def tile_attend_maxsim_ts_kernel(tc, qT, k_words, k_scales, ts, offs, out):
         for g in range(HALF_GROUPS):
             for b in range(BLOCKS):
                 multiply(g, b, 0, ALL_QUERIES[0], True, False)
+        multiply(HALF_GROUPS, 0, 0, ALL_QUERIES[0], True, False)
         for b in range(BLOCKS):
             for g in range(HALF_GROUPS):
                 multiply(g, b, 1, ALL_QUERIES[0], False, True)
         nc.vector.tensor_tensor(joined[1][:], joined[0][:], joined[1][:], MAX)
         for g in range(HALF_GROUPS, GROUPS):
             for b in range(BLOCKS):
-                multiply(g, b, 1, ALL_QUERIES[0], True, False)
-                multiply(g, b, 0, ALL_QUERIES[0], False, True)
+                if (g, b) == (HALF_GROUPS, 0):
+                    multiply(g, b, 1, ALL_QUERIES[0], False, True)
+                else:
+                    multiply(g, b, 1, ALL_QUERIES[0], True, False)
+                    multiply(g, b, 0, ALL_QUERIES[0], False, True)
 
         result = keep.tile([P, QT, GROUPS * GROUP_PASSAGES], F32, name="result")
         for g, first, run in ((1, 0, 16), (2, 8, 32), (3, 12, 32)):

@@ -22,26 +22,24 @@ D = 1024
 NQ = 256
 PASSAGE = 64
 PACK = 4
+ENTRIES = 16
 K_PASS = P * PACK
 PASSES = D // K_PASS
 SCALE_ROWS = K_PASS // 32
 QUAD_ROWS = SCALE_ROWS * QUADRANT // P
 HALVES = 2
 HALF = SLOTS // HALVES
-HALF_COLS = HALF // 16
-GROUPS = 4
-HALF_GROUPS = GROUPS // HALVES
-BLOCKS = SLOTS // GROUPS // P
-RUN = PASSAGE // BLOCKS
-GROUP_PASSAGES = P // RUN
-HALF_BLOCKS = HALF // P
-SHARING = (4, 2)
-GROUP = SLOTS // GROUPS
+HALF_COLS = HALF // ENTRIES
+HALF_TILES = HALF // P
+PAIR = 2
+PAIR_SLOTS = PAIR * P
+PAIRS = SLOTS // PAIR_SLOTS
+HALF_PAIRS = PAIRS // HALVES
+SHARING = (HALF_TILES, PAIR)
 QT = NQ // P
 RAW_BYTES = 4 * PACK * NQ
-KEY_BYTES = 2 * HALF
-ALL_QUERIES = (slice(0, NQ),)
-BY_QUERY_TILE = tuple(slice(t * P, (t + 1) * P) for t in range(QT))
+PAIR_BYTES = 4 * PAIR_SLOTS
+QUERY_TILES = tuple(slice(t * P, (t + 1) * P) for t in range(QT))
 
 FLOPS = 2 * NQ * SLOTS * D
 BYTES = (
@@ -49,7 +47,7 @@ BYTES = (
     + 4 * P * POOL
     + PASSES * SCALE_ROWS * POOL
     + 4 * POOL
-    + 2 * P * SLOTS // 16
+    + 2 * P * SLOTS // ENTRIES
     + 4 * NQ * SLOTS // PASSAGE
 )
 
@@ -59,7 +57,10 @@ def tile_attend_maxsim_ts_kernel(tc, qT, k_words, k_scales, ts, offs, out):
     with ExitStack() as ctx:
         keep = ctx.enter_context(tc.tile_pool(name="keep", bufs=1))
         reuse = ctx.enter_context(tc.tile_pool(name="reuse", bufs=1))
-        sums = ctx.enter_context(tc.psum_pool(name="sums", bufs=1))
+        banks = ctx.enter_context(tc.psum_pool(name="banks", bufs=1))
+
+        def bank(n, shape):
+            return banks.tile(shape, F32, name="bank%d" % n)
 
         def load_queries(o):
             raw = reuse.tile([P, PACK, NQ], F32, name="q_raw%d" % o, align_bytes=64, offset=RAW_BYTES * o)
@@ -68,22 +69,28 @@ def tile_attend_maxsim_ts_kernel(tc, qT, k_words, k_scales, ts, offs, out):
             )
             return raw
 
-        def paired(grouped, raw, cols):
+        def interleaving(grouped, raw, cols):
             return (
                 grouped[:, cols, :].rearrange("p (c i) j -> p c j i", i=2),
                 raw[:, :, cols].rearrange("p j (c i) -> p c j i", i=2),
             )
 
-        def quantise(o, grouped, tag, pieces):
-            codes = keep.tile([P, NQ], U32, name="q_codes%d" % o, tag=tag, align_bytes=64)
+        def quantise(o, grouped):
+            codes = keep.tile([P, NQ], U32, name="q_codes%d" % o, align_bytes=64)
             scales = keep.tile([P, NQ], U8, name="q_scales%d" % o, align_bytes=64)
-            for cols in pieces:
-                nc.vector.quantize_mx(
-                    out=codes[:, cols].bitcast(FP8X4),
-                    scales=scales[:, cols],
-                    in_=grouped[:, cols, :].rearrange("p w j -> p (w j)"),
-                )
+            nc.vector.quantize_mx(
+                out=codes[:].bitcast(FP8X4),
+                scales=scales[:],
+                in_=grouped[:].rearrange("p w j -> p (w j)"),
+            )
             return codes, scales
+
+        def tile_order(ordered, listed, h, run):
+            sizes = {"b": SHARING[h], "j": P * SHARING[h] // PASSAGE, "r": run}
+            return (
+                ordered.rearrange("p (g b j r) -> p g b j r", **sizes),
+                listed.rearrange("p (g j b r) -> p g b j r", **sizes),
+            )
 
         scale_pool = keep.tile([P, POOL], U8, name="scale_pool", align_bytes=64)
         nc.sync.dma_start(
@@ -92,10 +99,10 @@ def tile_attend_maxsim_ts_kernel(tc, qT, k_words, k_scales, ts, offs, out):
         )
         ts_pool = keep.tile([P, POOL], F32, name="ts_pool", align_bytes=64)
         nc.sync.dma_start(ts_pool[P - 1 : P, :], ts[0:1, :])
-        offsets = keep.tile([P, SLOTS // 16], U16, name="offsets")
+        offsets = keep.tile([P, SLOTS // ENTRIES], U16, name="offsets")
         nc.sync.dma_start(offsets[:], offs)
         q_raw = [load_queries(0)]
-        word_pool = keep.tile([P, POOL], I32, name="word_pool", tag="word_pool", align_bytes=64)
+        word_pool = keep.tile([P, POOL], I32, name="word_pool", align_bytes=64)
         nc.sync.dma_start(word_pool[:], k_words[0].rearrange("p t b -> p (t b)").bitcast(I32))
 
         nc.vector.memset(scale_pool[QUADRANT : 2 * QUADRANT, :].bitcast(I32), 0)
@@ -110,140 +117,132 @@ def tile_attend_maxsim_ts_kernel(tc, qT, k_words, k_scales, ts, offs, out):
         nc.gpsimd.iota(distance[:], [[-1, P]], base=0, channel_multiplier=1)
         identity = keep.tile([P, P], F32, name="identity")
         nc.vector.tensor_scalar(identity[:], distance[:], 0, None, mybir.AluOpType.is_equal)
-
-
-        def block_order(dst, src, h, per_slot):
-            blocks = SHARING[h]
-            run = PASSAGE // blocks // per_slot
-            cols = slice(h * HALF // per_slot, (h + 1) * HALF // per_slot)
-            return (
-                dst[:, cols].rearrange("p (g b j r) -> p g b j r", b=blocks, j=P * blocks // PASSAGE, r=run),
-                src[:, cols].rearrange("p (g j b r) -> p g b j r", b=blocks, j=P * blocks // PASSAGE, r=run),
-            )
-
         for h in range(HALVES):
-            nc.vector.tensor_copy(*block_order(planes[0][:].bitcast(I32), scale_listed[:].bitcast(I32), h, 4))
-
-        def place_scale_rows(o):
-            for quad in range(P // QUADRANT):
-                first = SCALE_ROWS * o + QUAD_ROWS * quad
-                if first:
-                    queue = nc.gpsimd if first == PASSES * SCALE_ROWS - QUAD_ROWS else nc.sync
-                    queue.dma_start(
-                        planes[o][QUADRANT * quad : QUADRANT * quad + QUAD_ROWS, :].bitcast(I32),
-                        planes[0][first : first + QUAD_ROWS, :].bitcast(I32),
-                    )
+            cols = slice(h * HALF, (h + 1) * HALF)
+            nc.vector.tensor_copy(
+                *tile_order(
+                    planes[0][:, cols].bitcast(I32),
+                    scale_listed[:, cols].bitcast(I32),
+                    h,
+                    PASSAGE // SHARING[h] // 4,
+                )
+            )
 
         q_raw.append(load_queries(1))
-        place_scale_rows(0)
-        place_scale_rows(1)
-
-        ts_blocks = [keep.tile([P, HALF], F32, name="ts_blocks%d" % h, align_bytes=64) for h in range(HALVES)]
-        for h in range(HALVES):
-            blocks = SHARING[h]
-            nc.vector.tensor_copy(
-                ts_blocks[h][:]
-                .bitcast(U32)
-                .rearrange("p (g b j r) -> p g j b r", b=blocks, j=P * blocks // PASSAGE, r=PASSAGE // blocks),
-                ts_pool[:].bitcast(U32).indirect(offsets[:, h * HALF_COLS : (h + 1) * HALF_COLS]),
+        for first in range(QUAD_ROWS, PASSES * SCALE_ROWS, QUAD_ROWS):
+            o, quad = first // SCALE_ROWS, first % SCALE_ROWS // QUAD_ROWS
+            queue = nc.gpsimd if first + QUAD_ROWS == PASSES * SCALE_ROWS else nc.sync
+            queue.dma_start(
+                planes[o][QUADRANT * quad : QUADRANT * quad + QUAD_ROWS, :].bitcast(I32),
+                planes[0][first : first + QUAD_ROWS, :].bitcast(I32),
             )
 
-        q_bf = [keep.tile([P, NQ, PACK], BF16, name="q_bf%d" % o, align_bytes=64) for o in range(PASSES)]
-        nc.scalar.activation(*paired(q_bf[0], q_raw[0], ALL_QUERIES[0]), COPY)
-        queries = [quantise(0, q_bf[0], "q_codes0", ALL_QUERIES)]
+        ts_ordered = [keep.tile([P, HALF], F32, name="ts_ordered%d" % h, align_bytes=64) for h in range(HALVES)]
+        nc.vector.tensor_copy(
+            ts_ordered[0][:].bitcast(U32).rearrange("p (b j r) -> p j b r", b=SHARING[0], r=PASSAGE // SHARING[0]),
+            ts_pool[:].bitcast(U32).indirect(offsets[:, 0:HALF_COLS]),
+        )
 
-        ts_col = keep.tile([P, HALVES, HALF_BLOCKS], F32, name="ts_col")
+        q_bf = [keep.tile([P, NQ, PACK], BF16, name="q_bf%d" % o, align_bytes=64) for o in range(PASSES)]
+        nc.scalar.activation(*interleaving(q_bf[0], q_raw[0], slice(0, NQ)), COPY)
+        queries = [quantise(0, q_bf[0])]
+
+        ts_listed = reuse.tile([P, HALF], F32, name="ts_listed", align_bytes=64, offset=0)
+        nc.scalar.activation(ts_listed[:], ts_pool[:].indirect(offsets[:, HALF_COLS : 2 * HALF_COLS]), COPY)
+        nc.scalar.copy(*tile_order(ts_ordered[1][:], ts_listed[:], 1, PASSAGE // SHARING[1]))
+
+        ts_col = reuse.tile([P, HALVES, HALF_TILES], F32, name="ts_col", align_bytes=64, offset=0)
         for h in range(HALVES):
-            turned = sums.tile([P, HALF_BLOCKS, P], F32, name="sum%d" % (6 + h))
-            for k in range(HALF_BLOCKS):
-                nc.tensor.transpose(turned[:, k, :], ts_blocks[h][:, k * P : (k + 1) * P], identity[:])
+            turned = bank(HALVES - 1 - h, [P, HALF_TILES, P])
+            for k in range(HALF_TILES):
+                nc.tensor.transpose(turned[:, k, :], ts_ordered[h][:, k * P : (k + 1) * P], identity[:])
             nc.scalar.copy(ts_col[:, h, :], turned[:, :, P - 1])
 
-        nc.scalar.activation(*paired(q_bf[1], q_raw[1], BY_QUERY_TILE[1]), COPY)
+        nc.scalar.activation(*interleaving(q_bf[1], q_raw[1], QUERY_TILES[1]), COPY)
 
         key_codes = {}
 
-        def gather_words(name, first, slots, blocks, pool, offset):
+        def gather_words(name, first_slot, slots, pool, offset):
             listed = pool.tile([P, slots], U32, name=name, align_bytes=64, offset=offset)
             nc.vector.tensor_copy(
                 listed[:],
-                word_pool[:].bitcast(U32).indirect(offsets[:, first // 16 : (first + slots) // 16]),
+                word_pool[:].bitcast(U32).indirect(offsets[:, first_slot // ENTRIES : (first_slot + slots) // ENTRIES]),
             )
             return listed[:].bitcast(U16).rearrange(
-                "p (j b r o) -> p o b j r", b=blocks, r=PASSAGE // blocks, o=PASSES
+                "p (j b r o) -> p o b j r", b=slots // P, r=PASSAGE * P // slots, o=PASSES
             )
 
-        def part(name, words, first, passes, pool, offset):
-            blocks, run = words.shape[2], words.shape[4]
-            codes = pool.tile([P, len(passes), blocks, P], U16, name=name, align_bytes=64, offset=offset)
+        def part(name, words, first_tile, passes, pool, offset):
+            tiles, run = words.shape[2], words.shape[4]
+            codes = pool.tile([P, len(passes), tiles, P], U16, name=name, align_bytes=64, offset=offset)
             nc.vector.tensor_copy(codes[:].rearrange("p o b (j r) -> p o b j r", r=run), words)
             for i, o in enumerate(passes):
-                for b in range(blocks):
-                    key_codes[(first + b, o)] = codes[:, i, b, :]
+                for b in range(tiles):
+                    key_codes[(first_tile + b, o)] = codes[:, i, b, :]
 
-        words0 = gather_words("words0", 0, HALF, HALF_BLOCKS, keep, None)
-        words2 = gather_words("words2", HALF, GROUP, BLOCKS, keep, None)
-        part("keys00", words0[:, 0:1, 0:BLOCKS], 0, (0,), keep, None)
-        part("keys01", words0[:, 0:1, BLOCKS:HALF_BLOCKS], BLOCKS, (0,), keep, None)
-        part("keys1", words0[:, 1:2], 0, (1,), keep, None)
-        nc.vector.tensor_copy(*paired(q_bf[1], q_raw[1], BY_QUERY_TILE[0]))
-        part("keys2", words2, HALF_BLOCKS, (0, 1), reuse, RAW_BYTES + KEY_BYTES)
-        queries.append(quantise(1, q_bf[1], "q_codes1", ALL_QUERIES))
-        words3 = gather_words("words3", HALF + GROUP, GROUP, BLOCKS, reuse, RAW_BYTES)
-        part("keys3", words3, HALF_BLOCKS + BLOCKS, (0, 1), keep, None)
+        words_half = gather_words("words_half", 0, HALF, keep, None)
+        words_third = gather_words("words_third", HALF, PAIR_SLOTS, keep, None)
+        for g in range(HALF_PAIRS):
+            part("keys_pair%d" % g, words_half[:, 0:1, PAIR * g : PAIR * (g + 1)], PAIR * g, (0,), keep, None)
+        part("keys_half", words_half[:, 1:2], 0, (1,), keep, None)
+        nc.vector.tensor_copy(*interleaving(q_bf[1], q_raw[1], QUERY_TILES[0]))
+        part("keys_third", words_third, HALF_TILES, (0, 1), reuse, RAW_BYTES + PAIR_BYTES)
+        queries.append(quantise(1, q_bf[1]))
+        words_last = gather_words("words_last", HALF + PAIR_SLOTS, PAIR_SLOTS, reuse, RAW_BYTES)
+        part("keys_last", words_last, HALF_TILES + PAIR, (0, 1), keep, None)
 
         scores = {}
         joined = {}
 
-        def multiply(g, b, o, cols, start, stop):
+        def multiply(g, b, o):
             q_codes, q_scales = queries[o]
-            n = BLOCKS * g + b
-            first = n * P
-            if start:
-                scores[(g, b)] = sums.tile([P, NQ], F32, name="sum%d" % n)
+            n = PAIR * g + b
+            opens = n not in scores
+            if opens:
+                scores[n] = bank(n, [P, NQ])
             nc.tensor.matmul_mx(
-                out=scores[(g, b)][:, cols],
+                out=scores[n][:],
                 lhsT=key_codes[(n, o)].bitcast(FP4X4),
-                lhsT_scale=planes[o][:, first : first + P],
-                rhs=q_codes[:, cols].bitcast(FP8X4),
-                rhs_scale=q_scales[:, cols],
-                start=start,
-                stop=stop,
+                lhsT_scale=planes[o][:, n * P : (n + 1) * P],
+                rhs=q_codes[:].bitcast(FP8X4),
+                rhs_scale=q_scales[:],
+                start=opens,
+                stop=not opens,
             )
-            if stop:
-                factor = ts_col[:, n // HALF_BLOCKS, n % HALF_BLOCKS : n % HALF_BLOCKS + 1]
-                dealt = scores[(g, b)][:].rearrange("p (m t) -> p t m", t=QT)
+            if not opens:
+                factor = ts_col[:, n // HALF_TILES, n % HALF_TILES : n % HALF_TILES + 1]
+                dealt = scores[n][:].rearrange("p (m t) -> p t m", t=QT)
                 if b == 0:
-                    joined[g] = keep.tile([P, QT, P], F32, name="best%d" % g)
+                    joined[g] = keep.tile([P, QT, P], F32, name="joined%d" % g)
                     nc.scalar.activation(joined[g][:], dealt, COPY, scale=factor)
                 else:
                     nc.vector.scalar_tensor_tensor(joined[g][:], dealt, factor, joined[g][:], MULT, MAX)
 
-        for g in range(HALF_GROUPS):
-            for b in range(BLOCKS):
-                multiply(g, b, 0, ALL_QUERIES[0], True, False)
-        multiply(HALF_GROUPS, 0, 0, ALL_QUERIES[0], True, False)
-        for b in range(BLOCKS):
-            for g in range(HALF_GROUPS):
-                multiply(g, b, 1, ALL_QUERIES[0], False, True)
+        for g in range(HALF_PAIRS):
+            for b in range(PAIR):
+                multiply(g, b, 0)
+        multiply(HALF_PAIRS, 0, 0)
+        for b in range(PAIR):
+            for g in range(HALF_PAIRS):
+                multiply(g, b, 1)
         nc.vector.tensor_tensor(joined[1][:], joined[0][:], joined[1][:], MAX)
-        for g in range(HALF_GROUPS, GROUPS):
-            for b in range(BLOCKS):
-                if (g, b) == (HALF_GROUPS, 0):
-                    multiply(g, b, 1, ALL_QUERIES[0], False, True)
-                else:
-                    multiply(g, b, 1, ALL_QUERIES[0], True, False)
-                    multiply(g, b, 0, ALL_QUERIES[0], False, True)
+        multiply(HALF_PAIRS, 0, 1)
+        for n in range(HALF_TILES + 1, PAIR * PAIRS):
+            for o in reversed(range(PASSES)):
+                multiply(n // PAIR, n % PAIR, o)
 
-        result = keep.tile([P, QT, GROUPS * GROUP_PASSAGES], F32, name="result")
-        for g, first, run in ((1, 0, 16), (2, 8, 32), (3, 12, 32)):
-            turned = sums.tile([P, QT, P], F32, name="sum%d" % (4 if g == 1 else 6 if g == 2 else 7))
+        result = keep.tile([P, QT, SLOTS // PASSAGE], F32, name="result")
+        first_passage = 0
+        for g, free_bank in ((1, HALF_TILES), (2, HALF_TILES + PAIR), (3, PAIR * PAIRS - 1)):
+            run = PASSAGE // SHARING[g // HALF_PAIRS]
+            turned = bank(free_bank, [P, QT, P])
             for t in range(QT):
                 nc.tensor.transpose(turned[:, t, :], joined[g][:, t, :], identity[:])
             nc.vector.tensor_reduce(
-                result[:, :, first : first + P // run],
+                result[:, :, first_passage : first_passage + P // run],
                 turned[:].rearrange("p t (j r) -> p t j r", r=run),
                 mybir.AxisListType.X,
                 MAX,
             )
+            first_passage = first_passage + P // run
         nc.sync.dma_start(out[0].rearrange("(p t) j -> p t j", p=P), result[:])

@@ -35,10 +35,11 @@ PAIR = 2
 PAIR_SLOTS = PAIR * P
 PAIRS = SLOTS // PAIR_SLOTS
 HALF_PAIRS = PAIRS // HALVES
-SHARING = (HALF_TILES, PAIR)
+SHARING = (PAIR, PAIR)
 QT = NQ // P
 RAW_BYTES = 4 * PACK * NQ
 PAIR_BYTES = 4 * PAIR_SLOTS
+LAST_PAIR = SLOTS - PAIR_SLOTS
 QUERY_TILES = tuple(slice(t * P, (t + 1) * P) for t in range(QT))
 
 FLOPS = 2 * NQ * SLOTS * D
@@ -97,68 +98,71 @@ def tile_attend_maxsim_ts_kernel(tc, qT, k_words, k_scales, ts, offs, out):
             scale_pool[0:QUADRANT, :].bitcast(I32),
             k_scales.rearrange("o f t -> (o f) t").bitcast(I32),
         )
-        ts_pool = keep.tile([P, POOL], F32, name="ts_pool", align_bytes=64)
-        nc.sync.dma_start(ts_pool[P - 1 : P, :], ts[0:1, :])
         offsets = keep.tile([P, SLOTS // ENTRIES], U16, name="offsets")
         nc.sync.dma_start(offsets[:], offs)
+        ts_pool = keep.tile([P, POOL], F32, name="ts_pool", align_bytes=64)
+        nc.sync.dma_start(ts_pool[P - 1 : P, :], ts[0:1, :])
         q_raw = [load_queries(0)]
         word_pool = keep.tile([P, POOL], I32, name="word_pool", align_bytes=64)
         nc.sync.dma_start(word_pool[:], k_words[0].rearrange("p t b -> p (t b)").bitcast(I32))
 
+        distance = keep.tile([P, P], F32, name="distance")
+        nc.gpsimd.iota(distance[:], [[-1, P]], base=0, channel_multiplier=1, allow_small_or_imprecise_dtypes=True)
+        zero = keep.tile([P, 1], F32, name="zero")
+        nc.vector.memset(zero[:], 0.0)
+        one = keep.tile([P, 1], F32, name="one")
+        nc.scalar.activation(one[:], zero[:], mybir.ActivationFunctionType.Identity, bias=1.0)
+        squared = keep.tile([P, P], F32, name="squared")
+        nc.scalar.activation(squared[:], distance[:], mybir.ActivationFunctionType.Square)
+        identity = keep.tile([P, P], F32, name="identity")
+        nc.scalar.activation(identity[:], squared[:], mybir.ActivationFunctionType.Relu, bias=one[:], scale=-1.0)
         nc.vector.memset(scale_pool[QUADRANT : 2 * QUADRANT, :].bitcast(I32), 0)
         nc.vector.memset(scale_pool[2 * QUADRANT : P, :].bitcast(I32), 0)
-        nc.vector.memset(ts_pool[0 : P - 1, :], 0.0)
-        planes = [keep.tile([P, SLOTS], U8, name="plane%d" % o, align_bytes=64) for o in range(PASSES)]
+        nc.vector.memset(ts_pool[0 : P - 1, 0 : POOL // 2], 0.0)
+        q_bf = [keep.tile([P, NQ, PACK], BF16, name="q_bf%d" % o, align_bytes=64) for o in range(PASSES)]
+        nc.scalar.activation(*interleaving(q_bf[0], q_raw[0], slice(0, NQ)), COPY)
+        planes = [
+            pool.tile([P, SLOTS], U8, name="plane%d" % o, align_bytes=64, offset=offset)
+            for o, (pool, offset) in enumerate(((keep, None), (keep, None)))
+        ]
 
         scale_listed = keep.tile([P, SLOTS], U8, name="scale_listed", align_bytes=64)
         nc.vector.tensor_copy(scale_listed[:], scale_pool[:].indirect(offsets[:]))
         nc.vector.memset(planes[1][:].bitcast(I32), 0)
-        distance = keep.tile([P, P], I32, name="distance")
-        nc.gpsimd.iota(distance[:], [[-1, P]], base=0, channel_multiplier=1)
-        identity = keep.tile([P, P], F32, name="identity")
-        nc.vector.tensor_scalar(identity[:], distance[:], 0, None, mybir.AluOpType.is_equal)
-        for h in range(HALVES):
-            cols = slice(h * HALF, (h + 1) * HALF)
-            nc.vector.tensor_copy(
-                *tile_order(
-                    planes[0][:, cols].bitcast(I32),
-                    scale_listed[:, cols].bitcast(I32),
-                    h,
-                    PASSAGE // SHARING[h] // 4,
-                )
-            )
+        nc.vector.memset(ts_pool[0 : P - 1, POOL // 2 : 5 * POOL // 8], 0.0)
+        nc.vector.tensor_copy(
+            *tile_order(planes[0][:].bitcast(I32), scale_listed[:].bitcast(I32), 0, PASSAGE // PAIR // 4)
+        )
 
+        nc.vector.memset(ts_pool[0 : P - 1, 5 * POOL // 8 : POOL], 0.0)
         q_raw.append(load_queries(1))
+        ts_ordered = [
+            keep.tile([P, slots], F32, name="ts_ordered%d" % i, align_bytes=64)
+            for i, slots in enumerate((LAST_PAIR, PAIR_SLOTS))
+        ]
+        nc.vector.tensor_copy(
+            ts_ordered[0][:].bitcast(U32).rearrange("p (g b j r) -> p g j b r", g=PAIRS - 1, b=PAIR, r=PASSAGE // PAIR),
+            ts_pool[:].bitcast(U32).indirect(offsets[:, 0 : LAST_PAIR // ENTRIES]),
+        )
+
+        queries = [quantise(0, q_bf[0])]
+
+        ts_listed = reuse.tile([P, PAIR_SLOTS], F32, name="ts_listed", align_bytes=64, offset=0)
+        nc.scalar.activation(ts_listed[:], ts_pool[:].indirect(offsets[:, LAST_PAIR // ENTRIES : SLOTS // ENTRIES]), COPY)
+        nc.scalar.copy(*tile_order(ts_ordered[1][:], ts_listed[:], 1, PASSAGE // SHARING[1]))
+
         for first in range(QUAD_ROWS, PASSES * SCALE_ROWS, QUAD_ROWS):
             o, quad = first // SCALE_ROWS, first % SCALE_ROWS // QUAD_ROWS
-            queue = nc.gpsimd if first + QUAD_ROWS == PASSES * SCALE_ROWS else nc.sync
+            queue = nc.scalar if o == 0 else nc.sync
             queue.dma_start(
                 planes[o][QUADRANT * quad : QUADRANT * quad + QUAD_ROWS, :].bitcast(I32),
                 planes[0][first : first + QUAD_ROWS, :].bitcast(I32),
             )
 
-        ts_ordered = [keep.tile([P, HALF], F32, name="ts_ordered%d" % h, align_bytes=64) for h in range(HALVES)]
-        nc.vector.tensor_copy(
-            ts_ordered[0][:].bitcast(U32).rearrange("p (b j r) -> p j b r", b=SHARING[0], r=PASSAGE // SHARING[0]),
-            ts_pool[:].bitcast(U32).indirect(offsets[:, 0:HALF_COLS]),
-        )
-
-        q_bf = [keep.tile([P, NQ, PACK], BF16, name="q_bf%d" % o, align_bytes=64) for o in range(PASSES)]
-        nc.scalar.activation(*interleaving(q_bf[0], q_raw[0], slice(0, NQ)), COPY)
-        queries = [quantise(0, q_bf[0])]
-
-        ts_listed = reuse.tile([P, HALF], F32, name="ts_listed", align_bytes=64, offset=0)
-        nc.scalar.activation(ts_listed[:], ts_pool[:].indirect(offsets[:, HALF_COLS : 2 * HALF_COLS]), COPY)
-        nc.scalar.copy(*tile_order(ts_ordered[1][:], ts_listed[:], 1, PASSAGE // SHARING[1]))
-
-        ts_col = reuse.tile([P, HALVES, HALF_TILES], F32, name="ts_col", align_bytes=64, offset=0)
-        for h in range(HALVES):
-            turned = bank(HALVES - 1 - h, [P, HALF_TILES, P])
-            for k in range(HALF_TILES):
-                nc.tensor.transpose(turned[:, k, :], ts_ordered[h][:, k * P : (k + 1) * P], identity[:])
-            nc.scalar.copy(ts_col[:, h, :], turned[:, :, P - 1])
-
-        nc.scalar.activation(*interleaving(q_bf[1], q_raw[1], QUERY_TILES[1]), COPY)
+        ts_turned = [bank(PAIR * PAIRS - HALVES + h, [P, HALF_TILES, P]) for h in range(HALVES)]
+        ts_tiles = [share[:, first : first + P] for share in ts_ordered for first in range(0, share.shape[1], P)]
+        for n, ts_tile in enumerate(ts_tiles):
+            nc.tensor.transpose(ts_turned[n // HALF_TILES][:, n % HALF_TILES, :], ts_tile, identity[:])
 
         key_codes = {}
 
@@ -180,16 +184,20 @@ def tile_attend_maxsim_ts_kernel(tc, qT, k_words, k_scales, ts, offs, out):
                 for b in range(tiles):
                     key_codes[(first_tile + b, o)] = codes[:, i, b, :]
 
-        words_half = gather_words("words_half", 0, HALF, keep, None)
-        words_third = gather_words("words_third", HALF, PAIR_SLOTS, keep, None)
-        for g in range(HALF_PAIRS):
-            part("keys_pair%d" % g, words_half[:, 0:1, PAIR * g : PAIR * (g + 1)], PAIR * g, (0,), keep, None)
-        part("keys_half", words_half[:, 1:2], 0, (1,), keep, None)
+        words = [gather_words("words%d" % g, g * PAIR_SLOTS, PAIR_SLOTS, keep, None) for g in range(HALF_PAIRS)]
+        for o in range(PASSES):
+            for g in range(HALF_PAIRS):
+                part("keys%d_%d" % (g, o), words[g][:, o : o + 1], PAIR * g, (o,), keep, None)
+        nc.scalar.activation(*interleaving(q_bf[1], q_raw[1], QUERY_TILES[1]), COPY)
         nc.vector.tensor_copy(*interleaving(q_bf[1], q_raw[1], QUERY_TILES[0]))
-        part("keys_third", words_third, HALF_TILES, (0, 1), reuse, RAW_BYTES + PAIR_BYTES)
+        ts_col = reuse.tile([P, HALVES, HALF_TILES], F32, name="ts_col", align_bytes=64, offset=RAW_BYTES)
+        for h in range(HALVES):
+            nc.scalar.copy(ts_col[:, h, :], ts_turned[h][:, :, P - 1])
         queries.append(quantise(1, q_bf[1]))
-        words_last = gather_words("words_last", HALF + PAIR_SLOTS, PAIR_SLOTS, reuse, RAW_BYTES)
-        part("keys_last", words_last, HALF_TILES + PAIR, (0, 1), keep, None)
+        for g in range(HALF_PAIRS, PAIRS):
+            words.append(gather_words("words%d" % g, g * PAIR_SLOTS, PAIR_SLOTS, reuse, RAW_BYTES + (g - 1) * PAIR_BYTES))
+        for g in range(HALF_PAIRS, PAIRS):
+            part("keys%d" % g, words[g], PAIR * g, (0, 1), keep, None)
 
         scores = {}
         joined = {}
@@ -221,28 +229,24 @@ def tile_attend_maxsim_ts_kernel(tc, qT, k_words, k_scales, ts, offs, out):
         for g in range(HALF_PAIRS):
             for b in range(PAIR):
                 multiply(g, b, 0)
-        multiply(HALF_PAIRS, 0, 0)
         for b in range(PAIR):
             for g in range(HALF_PAIRS):
                 multiply(g, b, 1)
-        nc.vector.tensor_tensor(joined[1][:], joined[0][:], joined[1][:], MAX)
-        multiply(HALF_PAIRS, 0, 1)
-        for n in range(HALF_TILES + 1, PAIR * PAIRS):
-            for o in reversed(range(PASSES)):
-                multiply(n // PAIR, n % PAIR, o)
+        for b in range(PAIR):
+            for g in range(HALF_PAIRS, PAIRS):
+                for o in reversed(range(PASSES)):
+                    multiply(g, b, o)
 
         result = keep.tile([P, QT, SLOTS // PASSAGE], F32, name="result")
-        first_passage = 0
-        for g, free_bank in ((1, HALF_TILES), (2, HALF_TILES + PAIR), (3, PAIR * PAIRS - 1)):
-            run = PASSAGE // SHARING[g // HALF_PAIRS]
+        run = PASSAGE // PAIR
+        for g, free_bank in enumerate((6, 4, 5, 7)):
             turned = bank(free_bank, [P, QT, P])
             for t in range(QT):
                 nc.tensor.transpose(turned[:, t, :], joined[g][:, t, :], identity[:])
             nc.vector.tensor_reduce(
-                result[:, :, first_passage : first_passage + P // run],
+                result[:, :, g * P // run : (g + 1) * P // run],
                 turned[:].rearrange("p t (j r) -> p t j r", r=run),
                 mybir.AxisListType.X,
                 MAX,
             )
-            first_passage = first_passage + P // run
         nc.sync.dma_start(out[0].rearrange("(p t) j -> p t j", p=P), result[:])

@@ -178,11 +178,13 @@ def tile_attend_maxsim_ts_kernel(tc, qT, k_words, k_scales, ts, offs, out):
 
         def part(name, words, first_tile, passes, pool, offset):
             tiles, run = words.shape[2], words.shape[4]
-            codes = pool.tile([P, len(passes), tiles, P], U16, name=name, align_bytes=64, offset=offset)
-            nc.vector.tensor_copy(codes[:].rearrange("p o b (j r) -> p o b j r", r=run), words)
+            codes = pool.tile([P, tiles, len(passes), P], U16, name=name, align_bytes=64, offset=offset)
+            nc.vector.tensor_copy(
+                codes[:].rearrange("p b o (j r) -> p b o j r", r=run), words.rearrange("p o b j r -> p b o j r")
+            )
             for i, o in enumerate(passes):
                 for b in range(tiles):
-                    key_codes[(first_tile + b, o)] = codes[:, i, b, :]
+                    key_codes[(first_tile + b, o)] = codes[:, b, i, :]
 
         words = [gather_words("words%d" % g, g * PAIR_SLOTS, PAIR_SLOTS, keep, None) for g in range(HALF_PAIRS)]
         for o in range(PASSES):

@@ -55,6 +55,13 @@ BYTES = (
 
 def tile_attend_maxsim_ts_kernel(tc, qT, k_words, k_scales, ts, offs, out):
     nc = tc.nc
+    KB = 1024
+    TS_AT = 0
+    RAW_AT = (16 * KB, 20 * KB)
+    LISTED_AT = 25 * KB
+    SHARING = (HALF_TILES, PAIR)
+    VECTOR_QUERIES = 128
+    SCALE_LISTED_AT = 30 * KB
     with ExitStack() as ctx:
         keep = ctx.enter_context(tc.tile_pool(name="keep", bufs=1))
         reuse = ctx.enter_context(tc.tile_pool(name="reuse", bufs=1))
@@ -63,8 +70,11 @@ def tile_attend_maxsim_ts_kernel(tc, qT, k_words, k_scales, ts, offs, out):
         def bank(n, shape):
             return banks.tile(shape, F32, name="bank%d" % n)
 
+        def placed(shape, dtype, name, offset):
+            return reuse.tile(shape, dtype, name=name, align_bytes=64, offset=offset)
+
         def load_queries(o):
-            raw = reuse.tile([P, PACK, NQ], F32, name="q_raw%d" % o, align_bytes=64, offset=RAW_BYTES * o)
+            raw = placed([P, PACK, NQ], F32, "q_raw%d" % o, RAW_AT[o])
             nc.sync.dma_start(
                 raw[:], qT[0, K_PASS * o : K_PASS * (o + 1), :].rearrange("(p j) w -> p j w", j=PACK)
             )
@@ -86,8 +96,8 @@ def tile_attend_maxsim_ts_kernel(tc, qT, k_words, k_scales, ts, offs, out):
             )
             return codes, scales
 
-        def tile_order(ordered, listed, h, run):
-            sizes = {"b": SHARING[h], "j": P * SHARING[h] // PASSAGE, "r": run}
+        def tile_order(ordered, listed, h, per_slot):
+            sizes = {"b": SHARING[h], "j": P * SHARING[h] // PASSAGE, "r": PASSAGE // SHARING[h] // per_slot}
             return (
                 ordered.rearrange("p (g b j r) -> p g b j r", **sizes),
                 listed.rearrange("p (g j b r) -> p g b j r", **sizes),
@@ -100,57 +110,44 @@ def tile_attend_maxsim_ts_kernel(tc, qT, k_words, k_scales, ts, offs, out):
         )
         offsets = keep.tile([P, SLOTS // ENTRIES], U16, name="offsets")
         nc.sync.dma_start(offsets[:], offs)
-        ts_pool = keep.tile([P, POOL], F32, name="ts_pool", align_bytes=64)
+        ts_pool = placed([P, POOL], F32, "ts_pool", TS_AT)
         nc.sync.dma_start(ts_pool[P - 1 : P, :], ts[0:1, :])
-        q_raw = [load_queries(0)]
         word_pool = keep.tile([P, POOL], I32, name="word_pool", align_bytes=64)
         nc.sync.dma_start(word_pool[:], k_words[0].rearrange("p t b -> p (t b)").bitcast(I32))
+        q_raw = [load_queries(o) for o in range(PASSES)]
 
         distance = keep.tile([P, P], F32, name="distance")
         nc.gpsimd.iota(distance[:], [[-1, P]], base=0, channel_multiplier=1, allow_small_or_imprecise_dtypes=True)
-        zero = keep.tile([P, 1], F32, name="zero")
-        nc.vector.memset(zero[:], 0.0)
+        nc.vector.memset(ts_pool[0 : P - 1, 0:8], 0.0)
+        nc.scalar.activation(
+            ts_pool[0 : P - 1, POOL // 2 : POOL].rearrange("p (n c) -> p n c", c=8),
+            ts_pool[0 : P - 1, 0:8].unsqueeze(1).to_broadcast([P - 1, POOL // 16, 8]),
+            COPY,
+        )
         one = keep.tile([P, 1], F32, name="one")
-        nc.scalar.activation(one[:], zero[:], mybir.ActivationFunctionType.Identity, bias=1.0)
+        nc.vector.memset(one[:], 1.0)
         squared = keep.tile([P, P], F32, name="squared")
         nc.scalar.activation(squared[:], distance[:], mybir.ActivationFunctionType.Square)
         identity = keep.tile([P, P], F32, name="identity")
         nc.scalar.activation(identity[:], squared[:], mybir.ActivationFunctionType.Relu, bias=one[:], scale=-1.0)
         nc.vector.memset(scale_pool[QUADRANT : 2 * QUADRANT, :].bitcast(I32), 0)
         nc.vector.memset(scale_pool[2 * QUADRANT : P, :].bitcast(I32), 0)
-        nc.vector.memset(ts_pool[0 : P - 1, 0 : POOL // 2], 0.0)
-        q_bf = [keep.tile([P, NQ, PACK], BF16, name="q_bf%d" % o, align_bytes=64) for o in range(PASSES)]
-        nc.scalar.activation(*interleaving(q_bf[0], q_raw[0], slice(0, NQ)), COPY)
-        planes = [
-            pool.tile([P, SLOTS], U8, name="plane%d" % o, align_bytes=64, offset=offset)
-            for o, (pool, offset) in enumerate(((keep, None), (keep, None)))
-        ]
+        nc.vector.memset(ts_pool[0 : P - 1, 8 : POOL // 2], 0.0)
+        planes = [keep.tile([P, SLOTS], U8, name="plane0", align_bytes=64)]
 
-        scale_listed = keep.tile([P, SLOTS], U8, name="scale_listed", align_bytes=64)
-        nc.vector.tensor_copy(scale_listed[:], scale_pool[:].indirect(offsets[:]))
+        run = PASSAGE // PAIR
+        scale_listed = []
+        for h in range(HALVES):
+            listed = placed([P, HALF], U8, "scale_listed%d" % h, SCALE_LISTED_AT + h * 8 * HALF)
+            nc.vector.tensor_copy(listed[:], scale_pool[:].indirect(offsets[:, h * HALF_COLS : (h + 1) * HALF_COLS]))
+            scale_listed.append(listed)
+        for h in range(HALVES):
+            nc.vector.tensor_copy(
+                *tile_order(planes[0][:, h * HALF : (h + 1) * HALF].bitcast(I32), scale_listed[h][:].bitcast(I32), h, 4)
+            )
+
+        planes.append(placed([P, SLOTS], U8, "plane1", SCALE_LISTED_AT - SLOTS + HALF))
         nc.vector.memset(planes[1][:].bitcast(I32), 0)
-        nc.vector.memset(ts_pool[0 : P - 1, POOL // 2 : 5 * POOL // 8], 0.0)
-        nc.vector.tensor_copy(
-            *tile_order(planes[0][:].bitcast(I32), scale_listed[:].bitcast(I32), 0, PASSAGE // PAIR // 4)
-        )
-
-        nc.vector.memset(ts_pool[0 : P - 1, 5 * POOL // 8 : POOL], 0.0)
-        q_raw.append(load_queries(1))
-        ts_ordered = [
-            keep.tile([P, slots], F32, name="ts_ordered%d" % i, align_bytes=64)
-            for i, slots in enumerate((LAST_PAIR, PAIR_SLOTS))
-        ]
-        nc.vector.tensor_copy(
-            ts_ordered[0][:].bitcast(U32).rearrange("p (g b j r) -> p g j b r", g=PAIRS - 1, b=PAIR, r=PASSAGE // PAIR),
-            ts_pool[:].bitcast(U32).indirect(offsets[:, 0 : LAST_PAIR // ENTRIES]),
-        )
-
-        queries = [quantise(0, q_bf[0])]
-
-        ts_listed = reuse.tile([P, PAIR_SLOTS], F32, name="ts_listed", align_bytes=64, offset=0)
-        nc.scalar.activation(ts_listed[:], ts_pool[:].indirect(offsets[:, LAST_PAIR // ENTRIES : SLOTS // ENTRIES]), COPY)
-        nc.scalar.copy(*tile_order(ts_ordered[1][:], ts_listed[:], 1, PASSAGE // SHARING[1]))
-
         for first in range(QUAD_ROWS, PASSES * SCALE_ROWS, QUAD_ROWS):
             o, quad = first // SCALE_ROWS, first % SCALE_ROWS // QUAD_ROWS
             queue = nc.scalar if o == 0 else nc.sync
@@ -158,58 +155,68 @@ def tile_attend_maxsim_ts_kernel(tc, qT, k_words, k_scales, ts, offs, out):
                 planes[o][QUADRANT * quad : QUADRANT * quad + QUAD_ROWS, :].bitcast(I32),
                 planes[0][first : first + QUAD_ROWS, :].bitcast(I32),
             )
+        ts_ordered = []
+        for h, offset in enumerate((SCALE_LISTED_AT + 8 * HALF, LISTED_AT)):
+            ts_listed = placed([P, HALF], F32, "ts_listed%d" % h, offset)
+            nc.vector.tensor_copy(ts_listed[:], ts_pool[:].indirect(offsets[:, h * HALF_COLS : (h + 1) * HALF_COLS]))
+            ts_ordered.append(keep.tile([P, HALF], F32, name="ts_ordered%d" % h, align_bytes=64))
+            nc.scalar.copy(*tile_order(ts_ordered[h][:], ts_listed[:], h, 1))
 
         ts_turned = [bank(PAIR * PAIRS - HALVES + h, [P, HALF_TILES, P]) for h in range(HALVES)]
-        ts_tiles = [share[:, first : first + P] for share in ts_ordered for first in range(0, share.shape[1], P)]
-        for n, ts_tile in enumerate(ts_tiles):
-            nc.tensor.transpose(ts_turned[n // HALF_TILES][:, n % HALF_TILES, :], ts_tile, identity[:])
+        for h in range(HALVES):
+            for n in range(HALF_TILES):
+                nc.tensor.transpose(ts_turned[h][:, n, :], ts_ordered[h][:, n * P : (n + 1) * P], identity[:])
 
         key_codes = {}
 
-        def gather_words(name, first_slot, slots, pool, offset):
-            listed = pool.tile([P, slots], U32, name=name, align_bytes=64, offset=offset)
+        def gather_words(name, first, slots, offset):
+            listed = placed([P, slots], U32, name, offset)
             nc.vector.tensor_copy(
-                listed[:],
-                word_pool[:].bitcast(U32).indirect(offsets[:, first_slot // ENTRIES : (first_slot + slots) // ENTRIES]),
+                listed[:], word_pool[:].bitcast(U32).indirect(offsets[:, first // ENTRIES : (first + slots) // ENTRIES])
             )
-            return listed[:].bitcast(U16).rearrange(
-                "p (j b r o) -> p o b j r", b=slots // P, r=PASSAGE * P // slots, o=PASSES
-            )
+            tiles = slots // P
+            return listed[:].bitcast(U16).rearrange("p (j b r o) -> p b o j r", b=tiles, r=PASSAGE // tiles, o=PASSES)
 
         def part(name, words, first_tile, passes, pool, offset):
-            tiles, run = words.shape[2], words.shape[4]
+            tiles, piece = words.shape[1], words.shape[4]
             codes = pool.tile([P, tiles, len(passes), P], U16, name=name, align_bytes=64, offset=offset)
             nc.vector.tensor_copy(
-                codes[:].rearrange("p b o (j r) -> p b o j r", r=run), words.rearrange("p o b j r -> p b o j r")
+                codes[:].rearrange("p b o (j r) -> p b o j r", r=piece), words[:, :, passes[0] : passes[-1] + 1]
             )
             for i, o in enumerate(passes):
                 for b in range(tiles):
                     key_codes[(first_tile + b, o)] = codes[:, b, i, :]
 
-        words = [gather_words("words%d" % g, g * PAIR_SLOTS, PAIR_SLOTS, keep, None) for g in range(HALF_PAIRS)]
-        for o in range(PASSES):
-            for g in range(HALF_PAIRS):
-                part("keys%d_%d" % (g, o), words[g][:, o : o + 1], PAIR * g, (o,), keep, None)
-        nc.scalar.activation(*interleaving(q_bf[1], q_raw[1], QUERY_TILES[1]), COPY)
-        nc.vector.tensor_copy(*interleaving(q_bf[1], q_raw[1], QUERY_TILES[0]))
-        ts_col = reuse.tile([P, HALVES, HALF_TILES], F32, name="ts_col", align_bytes=64, offset=RAW_BYTES)
+        def interleave(o, offset):
+            grouped = placed([P, NQ, PACK], BF16, "q_bf%d" % o, offset)
+            nc.scalar.activation(*interleaving(grouped, q_raw[o], slice(VECTOR_QUERIES, NQ)), COPY)
+            nc.vector.tensor_copy(*interleaving(grouped, q_raw[o], slice(0, VECTOR_QUERIES)))
+            return grouped
+
+        words_a = gather_words("words_a", 0, HALF, TS_AT)
+        words_2 = gather_words("words_2", HALF, PAIR_SLOTS, TS_AT + 4 * HALF)
+        q_bf = [interleave(0, LISTED_AT - KB)]
+        part("keys_a0", words_a, 0, (0,), reuse, LISTED_AT + KB)
+        queries = [quantise(0, q_bf[0])]
+        q_bf.append(interleave(1, RAW_AT[0]))
+        part("keys_a1", words_a, 0, (1,), reuse, RAW_AT[0] + 2 * KB)
+        ts_col = placed([P, HALVES, HALF_TILES], F32, "ts_col", RAW_AT[1] + 2 * KB)
         for h in range(HALVES):
             nc.scalar.copy(ts_col[:, h, :], ts_turned[h][:, :, P - 1])
         queries.append(quantise(1, q_bf[1]))
-        for g in range(HALF_PAIRS, PAIRS):
-            words.append(gather_words("words%d" % g, g * PAIR_SLOTS, PAIR_SLOTS, reuse, RAW_BYTES + (g - 1) * PAIR_BYTES))
-        for g in range(HALF_PAIRS, PAIRS):
-            part("keys%d" % g, words[g], PAIR * g, (0, 1), keep, None)
+        words_3 = gather_words("words_3", LAST_PAIR, PAIR_SLOTS, RAW_AT[1])
+        part("keys_2", words_2, HALF_TILES, (0, 1), reuse, RAW_AT[1] + KB)
+        part("keys_3", words_3, HALF_TILES + PAIR, (0, 1), keep, None)
 
         scores = {}
         joined = {}
 
-        def multiply(g, b, o):
+        def multiply(n, o):
+            g, b = divmod(n, PAIR)
             q_codes, q_scales = queries[o]
-            n = PAIR * g + b
             opens = n not in scores
             if opens:
-                scores[n] = bank(n, [P, NQ])
+                scores[n] = bank(n - HALF_TILES if n in (5, 7) else n, [P, NQ])
             nc.tensor.matmul_mx(
                 out=scores[n][:],
                 lhsT=key_codes[(n, o)].bitcast(FP4X4),
@@ -228,26 +235,23 @@ def tile_attend_maxsim_ts_kernel(tc, qT, k_words, k_scales, ts, offs, out):
                 else:
                     nc.vector.scalar_tensor_tensor(joined[g][:], dealt, factor, joined[g][:], MULT, MAX)
 
-        for g in range(HALF_PAIRS):
-            for b in range(PAIR):
-                multiply(g, b, 0)
-        for b in range(PAIR):
-            for g in range(HALF_PAIRS):
-                multiply(g, b, 1)
-        for b in range(PAIR):
-            for g in range(HALF_PAIRS, PAIRS):
-                for o in reversed(range(PASSES)):
-                    multiply(g, b, o)
+        for n in range(HALF_TILES):
+            multiply(n, 0)
+        for n in (0, 2, 1, 3):
+            multiply(n, 1)
+        nc.vector.tensor_tensor(joined[0][:], joined[0][:], joined[1][:], MAX)
+        for n in (4, 6, 5, 7):
+            for o in reversed(range(PASSES)):
+                multiply(n, o)
 
         result = keep.tile([P, QT, SLOTS // PASSAGE], F32, name="result")
-        run = PASSAGE // PAIR
-        for g, free_bank in enumerate((6, 4, 5, 7)):
+        for g, free_bank, first, count in ((0, 6, 0, 8), (2, 4, 8, 4), (3, 5, 12, 4)):
             turned = bank(free_bank, [P, QT, P])
             for t in range(QT):
                 nc.tensor.transpose(turned[:, t, :], joined[g][:, t, :], identity[:])
             nc.vector.tensor_reduce(
-                result[:, :, g * P // run : (g + 1) * P // run],
-                turned[:].rearrange("p t (j r) -> p t j r", r=run),
+                result[:, :, first : first + count],
+                turned[:].rearrange("p t (j r) -> p t j r", j=count),
                 mybir.AxisListType.X,
                 MAX,
             )

@@ -89,11 +89,12 @@ def tile_attend_maxsim_ts_kernel(tc, qT, k_words, k_scales, ts, offs, out):
         def quantise(o, grouped):
             codes = keep.tile([P, NQ], U32, name="q_codes%d" % o, align_bytes=64)
             scales = keep.tile([P, NQ], U8, name="q_scales%d" % o, align_bytes=64)
-            nc.vector.quantize_mx(
-                out=codes[:].bitcast(FP8X4),
-                scales=scales[:],
-                in_=grouped[:].rearrange("p w j -> p (w j)"),
-            )
+            for cols in QUERY_TILES:
+                nc.vector.quantize_mx(
+                    out=codes[:, cols].bitcast(FP8X4),
+                    scales=scales[:, cols],
+                    in_=grouped[:, cols, :].rearrange("p w j -> p (w j)"),
+                )
             return codes, scales
 
         def tile_order(ordered, listed, h, per_slot):
@@ -211,22 +212,22 @@ def tile_attend_maxsim_ts_kernel(tc, qT, k_words, k_scales, ts, offs, out):
         scores = {}
         joined = {}
 
-        def multiply(n, o):
+        def multiply(n, o, cols, closes):
             g, b = divmod(n, PAIR)
             q_codes, q_scales = queries[o]
             opens = n not in scores
             if opens:
                 scores[n] = bank(n - HALF_TILES if n in (5, 7) else n, [P, NQ])
             nc.tensor.matmul_mx(
-                out=scores[n][:],
+                out=scores[n][:, cols],
                 lhsT=key_codes[(n, o)].bitcast(FP4X4),
                 lhsT_scale=planes[o][:, n * P : (n + 1) * P],
-                rhs=q_codes[:].bitcast(FP8X4),
-                rhs_scale=q_scales[:],
+                rhs=q_codes[:, cols].bitcast(FP8X4),
+                rhs_scale=q_scales[:, cols],
                 start=opens,
-                stop=not opens,
+                stop=closes,
             )
-            if not opens:
+            if closes:
                 factor = ts_col[:, n // HALF_TILES, n % HALF_TILES : n % HALF_TILES + 1]
                 dealt = scores[n][:].rearrange("p (m t) -> p t m", t=QT)
                 if b == 0:
@@ -235,14 +236,19 @@ def tile_attend_maxsim_ts_kernel(tc, qT, k_words, k_scales, ts, offs, out):
                 else:
                     nc.vector.scalar_tensor_tensor(joined[g][:], dealt, factor, joined[g][:], MULT, MAX)
 
-        for n in range(HALF_TILES):
-            multiply(n, 0)
-        for n in (0, 2, 1, 3):
-            multiply(n, 1)
+        every = slice(0, NQ)
+        for cols in QUERY_TILES:
+            for n in range(HALF_TILES):
+                multiply(n, 0, cols, False)
+        for cols in QUERY_TILES:
+            for n in (0, 2):
+                multiply(n, 1, cols, cols == QUERY_TILES[-1])
+        for n in (1, 3):
+            multiply(n, 1, every, True)
         nc.vector.tensor_tensor(joined[0][:], joined[0][:], joined[1][:], MAX)
         for n in (4, 6, 5, 7):
             for o in reversed(range(PASSES)):
-                multiply(n, o)
+                multiply(n, o, every, o == 0)
 
         result = keep.tile([P, QT, SLOTS // PASSAGE], F32, name="result")
         for g, free_bank, first, count in ((0, 6, 0, 8), (2, 4, 8, 4), (3, 5, 12, 4)):

from contextlib import ExitStack

import concourse.mybir as mybir

F32 = mybir.dt.float32
BF16 = mybir.dt.bfloat16
I32 = mybir.dt.int32
U32 = mybir.dt.uint32
U16 = mybir.dt.uint16
U8 = mybir.dt.uint8
FP8X4 = mybir.dt.float8_e4m3fn_x4
FP4X4 = mybir.dt.float4_e2m1fn_x4
COPY = mybir.ActivationFunctionType.Copy
MULT = mybir.AluOpType.mult
MAX = mybir.AluOpType.max

P = 128
QUADRANT = 32
POOL = 4096
SLOTS = 1024
D = 1024
NQ = 256
PASSAGE = 64
PACK = 4
ENTRIES = 16
K_PASS = P * PACK
PASSES = D // K_PASS
SCALE_ROWS = K_PASS // 32
QUAD_ROWS = SCALE_ROWS * QUADRANT // P
HALVES = 2
HALF = SLOTS // HALVES
HALF_COLS = HALF // ENTRIES
HALF_TILES = HALF // P
PAIR = 2
PAIR_SLOTS = PAIR * P
PAIRS = SLOTS // PAIR_SLOTS
HALF_PAIRS = PAIRS // HALVES
SHARING = (PAIR, PAIR)
QT = NQ // P
RAW_BYTES = 4 * PACK * NQ
PAIR_BYTES = 4 * PAIR_SLOTS
LAST_PAIR = SLOTS - PAIR_SLOTS
QUERY_TILES = tuple(slice(t * P, (t + 1) * P) for t in range(QT))

FLOPS = 2 * NQ * SLOTS * D
BYTES = (
    4 * D * NQ
    + 4 * P * POOL
    + PASSES * SCALE_ROWS * POOL
    + 4 * POOL
    + 2 * P * SLOTS // ENTRIES
    + 4 * NQ * SLOTS // PASSAGE
)


def tile_attend_maxsim_ts_kernel(tc, qT, k_words, k_scales, ts, offs, out):
    nc = tc.nc
    KB = 1024
    TS_AT = 0
    RAW_AT = (16 * KB, 20 * KB)
    LISTED_AT = 25 * KB
    SHARING = (HALF_TILES, PAIR)
    VECTOR_QUERIES = 128
    SCALE_LISTED_AT = 30 * KB
    with ExitStack() as ctx:
        keep = ctx.enter_context(tc.tile_pool(name="keep", bufs=1))
        reuse = ctx.enter_context(tc.tile_pool(name="reuse", bufs=1))
        banks = ctx.enter_context(tc.psum_pool(name="banks", bufs=1))

        def bank(n, shape):
            return banks.tile(shape, F32, name="bank%d" % n)

        def placed(shape, dtype, name, offset):
            return reuse.tile(shape, dtype, name=name, align_bytes=64, offset=offset)

        def load_queries(o):
            raw = placed([P, PACK, NQ], F32, "q_raw%d" % o, RAW_AT[o])
            nc.sync.dma_start(
                raw[:], qT[0, K_PASS * o : K_PASS * (o + 1), :].rearrange("(p j) w -> p j w", j=PACK)
            )
            return raw

        def interleaving(grouped, raw, cols):
            return (
                grouped[:, cols, :].rearrange("p (c i) j -> p c j i", i=2),
                raw[:, :, cols].rearrange("p j (c i) -> p c j i", i=2),
            )

        def quantise(o, grouped):
            codes = keep.tile([P, NQ], U32, name="q_codes%d" % o, align_bytes=64)
            scales = keep.tile([P, NQ], U8, name="q_scales%d" % o, align_bytes=64)
            for cols in QUERY_TILES:
                nc.vector.quantize_mx(
                    out=codes[:, cols].bitcast(FP8X4),
                    scales=scales[:, cols],
                    in_=grouped[:, cols, :].rearrange("p w j -> p (w j)"),
                )
            return codes, scales

        def tile_order(ordered, listed, h, per_slot):
            sizes = {"b": SHARING[h], "j": P * SHARING[h] // PASSAGE, "r": PASSAGE // SHARING[h] // per_slot}
            return (
                ordered.rearrange("p (g b j r) -> p g b j r", **sizes),
                listed.rearrange("p (g j b r) -> p g b j r", **sizes),
            )

        scale_pool = keep.tile([P, POOL], U8, name="scale_pool", align_bytes=64)
        nc.sync.dma_start(
            scale_pool[0:QUADRANT, :].bitcast(I32),
            k_scales.rearrange("o f t -> (o f) t").bitcast(I32),
        )
        offsets = keep.tile([P, SLOTS // ENTRIES], U16, name="offsets")
        nc.sync.dma_start(offsets[:], offs)
        ts_pool = placed([P, POOL], F32, "ts_pool", TS_AT)
        nc.sync.dma_start(ts_pool[P - 1 : P, :], ts[0:1, :])
        word_pool = keep.tile([P, POOL], I32, name="word_pool", align_bytes=64)
        nc.sync.dma_start(word_pool[:], k_words[0].rearrange("p t b -> p (t b)").bitcast(I32))
        q_raw = [load_queries(o) for o in range(PASSES)]

        distance = keep.tile([P, P], F32, name="distance")
        nc.gpsimd.iota(distance[:], [[-1, P]], base=0, channel_multiplier=1, allow_small_or_imprecise_dtypes=True)
        nc.vector.memset(ts_pool[0 : P - 1, 0:8], 0.0)
        nc.scalar.activation(
            ts_pool[0 : P - 1, POOL // 2 : POOL].rearrange("p (n c) -> p n c", c=8),
            ts_pool[0 : P - 1, 0:8].unsqueeze(1).to_broadcast([P - 1, POOL // 16, 8]),
            COPY,
        )
        one = keep.tile([P, 1], F32, name="one")
        nc.vector.memset(one[:], 1.0)
        squared = keep.tile([P, P], F32, name="squared")
        nc.scalar.activation(squared[:], distance[:], mybir.ActivationFunctionType.Square)
        identity = keep.tile([P, P], F32, name="identity")
        nc.scalar.activation(identity[:], squared[:], mybir.ActivationFunctionType.Relu, bias=one[:], scale=-1.0)
        nc.vector.memset(scale_pool[QUADRANT : 2 * QUADRANT, :].bitcast(I32), 0)
        nc.vector.memset(scale_pool[2 * QUADRANT : P, :].bitcast(I32), 0)
        nc.vector.memset(ts_pool[0 : P - 1, 8 : POOL // 2], 0.0)
        planes = [keep.tile([P, SLOTS], U8, name="plane0", align_bytes=64)]

        run = PASSAGE // PAIR
        scale_listed = []
        for h in range(HALVES):
            listed = placed([P, HALF], U8, "scale_listed%d" % h, SCALE_LISTED_AT + h * 8 * HALF)
            nc.vector.tensor_copy(listed[:], scale_pool[:].indirect(offsets[:, h * HALF_COLS : (h + 1) * HALF_COLS]))
            scale_listed.append(listed)
        for h in range(HALVES):
            nc.vector.tensor_copy(
                *tile_order(planes[0][:, h * HALF : (h + 1) * HALF].bitcast(I32), scale_listed[h][:].bitcast(I32), h, 4)
            )

        planes.append(placed([P, SLOTS], U8, "plane1", SCALE_LISTED_AT - SLOTS + HALF))
        nc.vector.memset(planes[1][:].bitcast(I32), 0)
        for first in range(QUAD_ROWS, PASSES * SCALE_ROWS, QUAD_ROWS):
            o, quad = first // SCALE_ROWS, first % SCALE_ROWS // QUAD_ROWS
            queue = nc.scalar if o == 0 else nc.sync
            queue.dma_start(
                planes[o][QUADRANT * quad : QUADRANT * quad + QUAD_ROWS, :].bitcast(I32),
                planes[0][first : first + QUAD_ROWS, :].bitcast(I32),
            )
        ts_ordered = []
        for h, offset in enumerate((SCALE_LISTED_AT + 8 * HALF, LISTED_AT)):
            ts_listed = placed([P, HALF], F32, "ts_listed%d" % h, offset)
            nc.vector.tensor_copy(ts_listed[:], ts_pool[:].indirect(offsets[:, h * HALF_COLS : (h + 1) * HALF_COLS]))
            ts_ordered.append(keep.tile([P, HALF], F32, name="ts_ordered%d" % h, align_bytes=64))
            nc.scalar.copy(*tile_order(ts_ordered[h][:], ts_listed[:], h, 1))

        ts_turned = [bank(PAIR * PAIRS - HALVES + h, [P, HALF_TILES, P]) for h in range(HALVES)]
        for h in range(HALVES):
            for n in range(HALF_TILES):
                nc.tensor.transpose(ts_turned[h][:, n, :], ts_ordered[h][:, n * P : (n + 1) * P], identity[:])

        key_codes = {}

        def gather_words(name, first, slots, offset):
            listed = placed([P, slots], U32, name, offset)
            nc.vector.tensor_copy(
                listed[:], word_pool[:].bitcast(U32).indirect(offsets[:, first // ENTRIES : (first + slots) // ENTRIES])
            )
            tiles = slots // P
            return listed[:].bitcast(U16).rearrange("p (j b r o) -> p b o j r", b=tiles, r=PASSAGE // tiles, o=PASSES)

        def part(name, words, first_tile, passes, pool, offset):
            tiles, piece = words.shape[1], words.shape[4]
            codes = pool.tile([P, tiles, len(passes), P], U16, name=name, align_bytes=64, offset=offset)
            nc.vector.tensor_copy(
                codes[:].rearrange("p b o (j r) -> p b o j r", r=piece), words[:, :, passes[0] : passes[-1] + 1]
            )
            for i, o in enumerate(passes):
                for b in range(tiles):
                    key_codes[(first_tile + b, o)] = codes[:, b, i, :]

        def interleave(o, offset):
            grouped = placed([P, NQ, PACK], BF16, "q_bf%d" % o, offset)
            nc.scalar.activation(*interleaving(grouped, q_raw[o], slice(VECTOR_QUERIES, NQ)), COPY)
            nc.vector.tensor_copy(*interleaving(grouped, q_raw[o], slice(0, VECTOR_QUERIES)))
            return grouped

        words_a = gather_words("words_a", 0, HALF, TS_AT)
        words_2 = gather_words("words_2", HALF, PAIR_SLOTS, TS_AT + 4 * HALF)
        q_bf = [interleave(0, LISTED_AT - KB)]
        part("keys_a0", words_a, 0, (0,), reuse, LISTED_AT + KB)
        queries = [quantise(0, q_bf[0])]
        q_bf.append(interleave(1, RAW_AT[0]))
        part("keys_a1", words_a, 0, (1,), reuse, RAW_AT[0] + 2 * KB)
        ts_col = placed([P, HALVES, HALF_TILES], F32, "ts_col", RAW_AT[1] + 2 * KB)
        for h in range(HALVES):
            nc.scalar.copy(ts_col[:, h, :], ts_turned[h][:, :, P - 1])
        queries.append(quantise(1, q_bf[1]))
        words_3 = gather_words("words_3", LAST_PAIR, PAIR_SLOTS, RAW_AT[1])
        part("keys_2", words_2, HALF_TILES, (0, 1), reuse, RAW_AT[1] + KB)
        part("keys_3", words_3, HALF_TILES + PAIR, (0, 1), keep, None)

        scores = {}
        joined = {}

        def multiply(n, o, cols, closes):
            g, b = divmod(n, PAIR)
            q_codes, q_scales = queries[o]
            opens = n not in scores
            if opens:
                scores[n] = bank(n - HALF_TILES if n in (5, 7) else n, [P, NQ])
            nc.tensor.matmul_mx(
                out=scores[n][:, cols],
                lhsT=key_codes[(n, o)].bitcast(FP4X4),
                lhsT_scale=planes[o][:, n * P : (n + 1) * P],
                rhs=q_codes[:, cols].bitcast(FP8X4),
                rhs_scale=q_scales[:, cols],
                start=opens,
                stop=closes,
            )
            if closes:
                factor = ts_col[:, n // HALF_TILES, n % HALF_TILES : n % HALF_TILES + 1]
                dealt = scores[n][:].rearrange("p (m t) -> p t m", t=QT)
                if b == 0:
                    joined[g] = keep.tile([P, QT, P], F32, name="joined%d" % g)
                    nc.scalar.activation(joined[g][:], dealt, COPY, scale=factor)
                else:
                    nc.vector.scalar_tensor_tensor(joined[g][:], dealt, factor, joined[g][:], MULT, MAX)

        every = slice(0, NQ)
        for cols in QUERY_TILES:
            for n in range(HALF_TILES):
                multiply(n, 0, cols, False)
        for cols in QUERY_TILES:
            for n in (0, 2):
                multiply(n, 1, cols, cols == QUERY_TILES[-1])
        for n in (1, 3):
            multiply(n, 1, every, True)
        nc.vector.tensor_tensor(joined[0][:], joined[0][:], joined[1][:], MAX)
        for n in (4, 6, 5, 7):
            for o in reversed(range(PASSES)):
                multiply(n, o, every, o == 0)

        result = keep.tile([P, QT, SLOTS // PASSAGE], F32, name="result")
        for g, free_bank, first, count in ((0, 6, 0, 8), (2, 4, 8, 4), (3, 5, 12, 4)):
            turned = bank(free_bank, [P, QT, P])
            for t in range(QT):
                nc.tensor.transpose(turned[:, t, :], joined[g][:, t, :], identity[:])
            nc.vector.tensor_reduce(
                result[:, :, first : first + count],
                turned[:].rearrange("p t (j r) -> p t j r", j=count),
                mybir.AxisListType.X,
                MAX,
            )
        nc.sync.dma_start(out[0].rearrange("(p t) j -> p t j", p=P), result[:])
